import numpy as np, ml_dtypes
CORES = [13,21,141,149]
N = 4
BF = ml_dtypes.bfloat16
def gentries(a):
    return np.ascontiguousarray(a.reshape(8, 16, -1).transpose(0, 2, 1)).reshape(8, -1)
def gtable(e):
    e = np.asarray(e); return np.ascontiguousarray(e.reshape(8, -1, 16).transpose(0, 2, 1)).reshape(128, -1).astype(np.int32)
W, L, M, B, TS, CAP = 4096, 256, 8, 2, 4, 96
R = M * B
KAPPA = (3, 29, 71, 113, 151, 197, 233, 277)
def run(x, z, v):
    tr = []
    for b in range(B):
        u = np.add.reduce(z, axis=2)
        c = np.concatenate([((u * u >> 4) + k * u + v) & (W - 1) for k in KAPPA], axis=2)
        y = np.take_along_axis(x, c[:, :, None, :], 3).reshape(N, 8, 16, M, L)
        z = np.abs(np.maximum.reduce(y, axis=3) - z)
        tr.append(c)
    return z, np.concatenate(tr, axis=2)
def starts(z, h, fr):
    halt = (~fr) & (np.add.reduce((z >= h[..., None]).astype(np.int64), axis=2) >= 9)
    slot = np.add.accumulate(halt.astype(np.int64), axis=2) - halt
    return halt & (slot < CAP)
def parts(rng):
    return rng.integers(0, 256, (N, 8, 16, W)), rng.integers(0, 256, (N, 8, 16, L)), rng.integers(0, W, (N, 8, L))
def levels(rng, x, s, v, share):
    j = rng.integers(-24, 25, (N, 8, 16, TS)); z = run(x, s, v)[0]; th = np.zeros((N, 8, 16, TS), np.int64)
    for t in range(TS):
        k = np.sort(np.sort(z - j[..., t:t + 1], axis=2)[:, :, 7], axis=2)
        n = np.minimum(np.maximum((share[..., t] * L).astype(np.int64), 1), L)
        th[..., t] = np.take_along_axis(k, (L - n)[..., None], 2) + j[..., t]
    return np.minimum(np.maximum(th, 0), 255)
def pack(x, s, v, th):
    return {"x": x.reshape(N, 128, W).astype(np.float32).astype(BF), "sd": s.reshape(N, 128, L).astype(np.float32).astype(BF),
            "v0": np.stack([gtable(a) for a in v]), "th": np.ascontiguousarray(th.reshape(N, 128, TS)).astype(np.int32)}
def shares(rng):
    return rng.choice(np.array([0.1, 0.25, 0.4, 0.6]), (N, 8, TS))
def setup_inputs(rng):
    x, s, v = parts(rng)
    return pack(x, s, v, levels(rng, x, s, v, shares(rng)))
def setup_inputs_claims(rng):
    x, s, v = parts(rng); share = rng.choice(np.array([0.2, 0.35, 0.45]), (N, 8, TS)); th = levels(rng, x, s, v, share)
    z, c = run(x, s, v); go = starts(z, th[..., 0], np.zeros((N, 8, L), bool))
    for r in range(0, N, 2):
        for g in range(8):
            j = np.nonzero(go[r + 1, g])[0]
            if len(j) == 0: j = np.arange(L)
            e = rng.choice(np.array([0, R - 1, -1]), L); e = np.where(e < 0, rng.integers(0, R, L), e)
            v[r, g] = np.where(rng.random(L) < 0.6, c[r + 1, g, e * L + rng.choice(j, L)], v[r, g])
    th[0::2] = levels(rng, x, s, v, share)[0::2]
    th[1, :, :, 1] = 255; th[:, 5, :, 2] = 255; th[2, :, :, TS - 1] = 255
    return pack(x, s, v, th)
def setup_inputs_corners(rng):
    x, s, v = parts(rng); v = np.ascontiguousarray(np.argsort(rng.random((N, 8, W)), axis=-1)[..., :L])
    pm = np.ones((N, 8), bool); pm[2:, 6:] = False
    x = np.where(pm[:, :, None, None], 255, x)
    n = rng.choice(np.array([0, 1, CAP - 1, CAP, CAP + 1, L]), (N, 8)); n[0] = 0
    n[1] = np.array([CAP, CAP + 1, L, CAP, L, CAP + 1, CAP, L]); n[2] = np.array([CAP, CAP + 1, L, CAP - 1, 1, 0, CAP, CAP])
    hot = np.argsort(np.argsort(rng.random((N, 8, L)), axis=2), axis=2) < n[:, :, None]
    k = np.where(hot, np.where(rng.random((N, 8, L)) < 0.5, 9, rng.integers(9, 17, (N, 8, L))), np.where(rng.random((N, 8, L)) < 0.5, 8, rng.integers(0, 9, (N, 8, L))))
    up = np.argsort(np.argsort(rng.random((N, 8, 16, L)), axis=2), axis=2) < k[:, :, None, :]
    tb = rng.integers(1, 256, (N, 8, 16)); tb[:, 1] = 1; tb[:, 3] = 255; tb[:, 5] = rng.choice(np.array([1, 255]), (N, 16))
    b = tb[..., None]; near = rng.random(s.shape) < 0.5
    hi = np.where(near, b, b + ((256 - b) * rng.random(s.shape)).astype(np.int64)); lo = np.where(near, b - 1, (b * rng.random(s.shape)).astype(np.int64))
    s = np.where(pm[:, :, None, None], np.where(up, hi, lo), s)
    th = levels(rng, x, s, v, shares(rng)); th[..., 0] = np.where(pm[:, :, None], tb, th[..., 0])
    return pack(x, s, v, th)
def setup_inputs_ends(rng):
    x, s, v = parts(rng); one = 1.0
    for i in range(M.bit_length() - 1): one = one * 0.5
    a = rng.random((N, 8, 1, W)); x = np.where(a < 0.4 * one, 255, np.where(a < 1.2 * one, 255 * rng.integers(0, 2, x.shape), 0))
    a = rng.random((N, 8, 1, L)); s = np.where(a < 0.35, 255, np.where(a < 0.6, 0, 255 * rng.integers(0, 2, s.shape)))
    v = np.where(rng.random(v.shape) < 0.72, (W - 1) * rng.integers(0, 2, v.shape), v)
    x[:, 1::2, :, W - 1] = 255; x[:, 0::2, :, W - 1] = 0; x[:, :, :, 0] = 255 - x[:, :, :, W - 1]
    s[:, 1::2, :, L - 1] = 255; s[:, 0::2, :, L - 1] = 0; s[:, :, :, 0] = 255 - s[:, :, :, L - 1]; s[:, 1::2, :, 5] = 255; s[:, 1::2, :, L - 4] = 255
    v[:, :, L - 1] = W - 1; v[:, :, L - 4] = W - 1; v[:, :, 5] = W - 1; v[:, :, 0] = 0
    k = rng.choice(np.array([16, 16, 12, 10, 9, 8, 8, 7, 0]), (N, 8, 1, TS)); k[:, 7, :, 0] = 12; k[:, 6, :, 0] = 0; k[:, 0, :, TS - 1] = 9; k[:, 7, :, TS - 1] = 16
    th = np.where(np.argsort(np.argsort(rng.random((N, 8, 16, TS)), axis=2), axis=2) < k, 255, 0)
    return pack(x, s, v, th)
def setup_inputs_spread(rng):
    x, s, v = parts(rng)
    x = np.minimum((np.exp2(1 + 7 * rng.random((N, 8, 1, W))) * rng.random(x.shape)).astype(np.int64), 255)
    s = np.minimum((np.exp2(1 + 7 * rng.random((N, 8, 1, L))) * rng.random(s.shape)).astype(np.int64), 255)
    v = np.minimum((W * rng.random(v.shape) ** 3).astype(np.int64), W - 1)
    return pack(x, s, v, levels(rng, x, s, v, shares(rng)))
def setup_inputs_ties(rng):
    x, s, v = parts(rng); pool = rng.integers(0, W, (8, 12)); pool[:, 0] = 0; pool[:, 1] = W - 1; h = L // 2; q = L // 4
    v = np.stack([pool[g][rng.integers(0, 12, (N, L))] for g in range(8)], axis=1)
    s[..., h:] = s[..., :h]; v[..., h:] = np.where(rng.random((N, 8, h)) < 0.5, v[..., :h], v[..., h:])
    pl = [2, 4, 7]; x[:, 2] = 255; x[:, 4] = 0; x[:, 7] = 0
    s[:, pl] = rng.integers(0, 100, (N, 3, 16, L))
    for a in range(0, N, 2):
        b = a + 1
        k = int(rng.integers(1, 4)); p = int(v[b, 2, 0])
        s[b, 2, :, k * q:(k + 1) * q] = 255; v[b, 2, k * q:(k + 1) * q] = p
        s[a, 2, :, (k - 1) * q:k * q] = rng.integers(201, 256, (16, q))
        v[a, 2, (k - 1) * q:k * q] = np.where(rng.random(q) < 0.8, p, v[a, 2, (k - 1) * q:k * q]); v[a, 2, (k - 1) * q] = p
        ln = np.append(q + rng.permutation(3 * q - 1)[:3], L - 1); e = rng.integers(201, 252, 4); pv = 16 * rng.permutation(W // 16)[:4] + 1; u = 16 * e
        s[b, 4][:, ln] = e; v[b, 4][ln] = pv
        wr = rng.permutation(q)[:4 * M]; s[a, 4][:, wr] = rng.integers(201, 252, 4 * M); s[a, 4][5, wr] += 4
        v[a, 4][wr] = np.concatenate([((u * u >> 4) + m * u + pv) & (W - 1) for m in KAPPA])
        p = W - 2 if a == 0 else int(rng.integers(W // 2, W - 1))
        for l, c in ((0, p + 1), (h, p)):
            s[b, 7, :, l] = rng.integers(201, 256, 16); u = int(np.sum(s[b, 7, :, l])); v[b, 7, l] = (c - (u * u >> 4) - KAPPA[0] * u) & (W - 1)
        for l, c in ((3, p + 1), (L - 1, p)):
            s[a, 7, :, l] = rng.integers(201, 256, 16); v[a, 7, l] = c
    th = levels(rng, x, s, v, shares(rng)); th[..., 0][:, pl] = rng.integers(100, 201, (N, 3, 16))
    return pack(x, s, v, th)
def check_inputs(d):
    bad = []
    for k, lo, hi in (("x", 0, 255), ("sd", 0, 255), ("v0", 0, W - 1), ("th", 0, 255)):
        a = np.asarray(d[k]).astype(np.float64)
        if not (np.min(a) >= lo and np.max(a) <= hi): bad.append("range of " + k)
        elif np.any(np.floor(a) != a): bad.append("whole numbers in " + k)
    return bad
def reference(x, sd, v0, th):
    X = x.astype(np.float32).astype(np.int64).reshape(N, 8, 16, W); S = sd.astype(np.float32).astype(np.int64).reshape(N, 8, 16, L)
    H = th.astype(np.int64).reshape(N, 8, 16, TS); v = np.stack([gentries(a) for a in v0]).astype(np.int64)
    fr = np.zeros((N, 8, L), bool); tr = np.zeros((N, 8, R * L), np.int64); cl = np.arange(L) * 4 // L
    for t in range(TS):
        z, c = run(X, S, v)
        tr = np.where(np.tile(fr, (1, 1, R)), tr, c)
        go = starts(z, H[..., t], fr); fr = fr | go
        back = np.zeros((N, 8, L), bool); hurt = np.zeros((N, 8, L), bool); done = np.zeros((N, 1, 1), np.int64)
        for q in range(N):
            p = q ^ (1 + t % (N - 1))
            for g in range(8):
                ln = np.nonzero(go[p, g])[0]; w = v[p, g, ln]
                mark = np.full(W, 9); np.minimum.at(mark, tr[q, g], np.where(np.tile(fr[q, g], R), np.tile(cl, R), 9))
                ok = np.nonzero(mark[w] > cl[ln])[0]
                win = np.zeros(len(ln), bool); win[ok[np.unique(w[ok], return_index=True)[1]]] = True
                back[p, g, ln[~win]] = True; done[q, 0, 0] += np.count_nonzero(win)
                if t < TS - 1: X[q, g][:, w[win]] = z[p, g][:, ln[win]]
                hit = np.zeros(W, bool); hit[w[win]] = True
                hurt[q, g] = fr[q, g] & np.any(hit[tr[q, g]].reshape(R, L), axis=0)
        fr = fr & (~back) & (~hurt)
        v = np.where(fr, v, (((v & 4095) ** 2 >> 3) + 37 * v + done) & (W - 1))
    ys = np.concatenate([v, fr.astype(np.int64)], axis=2)
    return {"yt": np.stack([gtable(a) for a in tr]).astype(np.float32), "ys": np.stack([gtable(a) for a in ys]).astype(np.float32)}

@@ -1,0 +1,650 @@
+from concourse.bass import DstId
+from concourse.mybir import AluOpType as OP, AxisListType, ActivationFunctionType as AF
+
+KAP = (3, 29, 71, 113, 151, 197, 233, 277)
+STAGES, CAP = 4, 96
+NE = 8
+DUMP = 4112
+NV, NSC = 48, 80
+SENT = 8191 * 256
+
+_F, _B, _I, _U = "float32", "bfloat16", "int32", "uint16"
+
+
+def _sb(n, d):
+    return ("sbuf", [128, n], d)
+
+
+SCRATCH = {
+    "xt": _sb(4224, _B), "D": _sb(4224, _B), "Z0": _sb(256, _B), "Z1": _sb(256, _B), "Z2": _sb(256, _B),
+    "V0": _sb(16, _I), "THI": _sb(4, _I), "THF": _sb(4, _F),
+    "GT": _sb(2048, _B), "HM": _sb(2048, _B), "SEG": _sb(1024, _B), "G2": _sb(4096, _B),
+    "CJ": _sb(128, _F), "GJ": _sb(128, _F), "GH": _sb(128, _F), "GM": _sb(128, _F), "TJ": _sb(128, _F),
+    "IS": _sb(96, _F), "K96": _sb(96, _F), "PI": _sb(1, _I), "PT": _sb(5, _I), "PC": _sb(5, _F), "DC": _sb(8, _F),
+    "BE": _sb(8, _F), "PQ": _sb(8, _F), "KROW": _sb(8, _F), "KEQ": _sb(8, _F), "KC": _sb(4, _F), "RI": _sb(16, _F),
+    "CLSR": _sb(256, _B), "DUMPP": _sb(128, _F), "DPT": _sb(128, _F),
+    "BO": _sb(128, _B), "BOK": _sb(128, _B), "WU0": _sb(128, _B), "WU1": _sb(128, _B), "ID": _sb(128, _B), "NI": _sb(128, _B),
+    "N32": _sb(128, _B), "M1K": _sb(128, _B), "RK1": _sb(128, _B), "RK2": _sb(128, _B), "RT1": _sb(128, _B), "RT2": _sb(128, _B),
+    "PL": _sb(1024, _B), "LP": _sb(1024, _B), "HS0": _sb(128, _B), "HS1": _sb(128, _B), "RS": _sb(2048, _B),
+    "VS0": _sb(128, _B), "VS1": _sb(128, _B), "E0": _sb(128, _B), "KR1": _sb(128, _B), "KR2": _sb(128, _B), "KR3": _sb(128, _B),
+    "ONE": _sb(256, _B), "ZER": _sb(128, _B), "DIAG": _sb(96, _F), "HOLD": _sb(96, _F), "RST": _sb(96, _F), "OB": _sb(96, _B),
+    "R0M": _sb(96, _F), "CODE": _sb(96, _B), "DMP6": _sb(6, _F), "W6": _sb(6, _F), "K8T": _sb(256, _F), "K2T": _sb(256, _F),
+    "YLI": _sb(32, _I), "YLU": _sb(32, _U),
+    "VH0": _sb(16, _B), "VL0": _sb(16, _B), "S0F": _sb(128, _F), "S0I": _sb(128, _I),
+    "CAT": _sb(384, _F), "CH": _sb(384, _B), "CL": _sb(384, _B), "U1": _sb(128, _F), "SQ": _sb(128, _F),
+    "TA": _sb(128, _I), "T1": _sb(128, _I), "TR": _sb(256, _I), "LU": _sb(256, _U), "VCI": _sb(128, _I), "VM": _sb(128, _F),
+    "VHI": _sb(128, _B), "VLO": _sb(128, _B), "GE": _sb(256, _B), "FL": _sb(128, _B), "INC": _sb(128, _B), "OFFP": _sb(128, _B),
+    "OL": _sb(16, _U), "XF": _sb(256, _F), "XW": _sb(1024, _I), "GO": _sb(128, _B), "FR": _sb(128, _B), "NF2": _sb(128, _B),
+    "P1": _sb(256, _I), "LG": _sb(256, _I), "LGU": _sb(256, _U), "WT": _sb(384, _F), "WI": _sb(128, _I), "ZS": _sb(128, _I),
+    "ZN": _sb(128, _I), "SEL": _sb(256, _F),
+    "XR": _sb(384, _I), "RR": _sb(32, _B), "MS": _sb(512, _I), "VWIN": _sb(1024, _B),
+    "E": _sb(336, _B), "FX": _sb(1152, _F), "N3": _sb(1024, _I), "DLU": _sb(12, _U), "DN": _sb(8, _B), "HB": _sb(256, _B),
+    "VROW": _sb(256, _B), "ACOL": _sb(4, _F), "UL": _sb(48, _F), "YO": _sb(256, _F), "YS": _sb(32, _F), "FIN": _sb(96, _F),
+}
+for _k in range(8):
+    SCRATCH["PB%d" % _k] = ("psum", [128, 512], "float32")
+
+SEMAPHORES = ["qv", "qs", "qp", "qg", "dx", "dsd", "dv0", "dth", "dyt", "dys"] + [n + str(t) for t in range(STAGES) for n in ("xin", "rin", "xl", "rl")]
+
+
+def _partner(r, t):
+    return r ^ (1 + t % 3)
+
+
+def _relay(c, T, topo):
+    r = T.rank_of(c)
+    far = [T.cores[_partner(r, t)] for t in range(STAGES)]
+    far = [d for d in far if not topo.may_write(c, d)]
+    if not far:
+        return None
+    ks = [k for k in topo.cores_of(c) if k not in T.cores and topo.may_write(c, k) and all(topo.may_write(k, d) for d in far)]
+    ks.sort(key=lambda k: (topo.die(k) != topo.die(c), k))
+    return ks[0]
+
+
+def _send(g, T, topo, src, dst, out, in_, rsem, lsem):
+    eng = [e for e in topo.engines(src, dst)][:NE]
+    m = 0
+    for e in eng:
+        m |= 1 << e
+    rid, pid = topo.addr(dst, src)
+    g.remote_dma(out, in_, remote_sem=T.sem[rsem], local_sem=T.sem[lsem], pid=pid, routing_id=rid, dma_engine_mask=m)
+
+
+def _relay_program(g, core, T, topo, c):
+    r = T.rank_of(c)
+    used = []
+    for t in range(STAGES):
+        d = T.cores[_partner(r, t)]
+        if topo.may_write(c, d):
+            continue
+        g.wait_ge(T.sem["xin%d" % t], NE)
+        _send(g, T, topo, core, d, T.XR[:, 96 * t:96 * t + 96], T.XR[:, 96 * t:96 * t + 96], "xin%d" % t, "xl%d" % t)
+        g.wait_ge(T.sem["rin%d" % t], NE)
+        _send(g, T, topo, core, d, T.RR[:, 8 * t:8 * t + 8], T.RR[:, 8 * t:8 * t + 8], "rin%d" % t, "rl%d" % t)
+        used.append(t)
+    for t in used:
+        g.wait_ge(T.sem["xl%d" % t], NE)
+        g.wait_ge(T.sem["rl%d" % t], NE)
+
+
+def rank_program(g, core, T, topo):
+    rank = T.rank_of(core)
+    if rank is None:
+        for c in T.cores:
+            if core in topo.cores_of(c) and _relay(c, T, topo) == core:
+                _relay_program(g, core, T, topo, c)
+        return
+
+    Q = {"v": g.vector, "s": g.scalar, "p": g.tensor, "g": g, "y": g.sync}
+    CNT = {"v": 0, "s": 0, "p": 0, "g": 0}
+    clk = {q: {} for q in Q}
+    acc = {}
+    idx = [0]
+
+    def X(name, a=0, b=None, st=1):
+        n = SCRATCH[name][1][1]
+        b = n if b is None else b
+        return (T[name][:, a:b:st] if st != 1 else T[name][:, a:b], [(name, a, b)])
+
+    def IND(win, off):
+        return (win[0].indirect(off[0]), win[1], off[1])
+
+    def wait(q, rec):
+        if clk[q].get(rec["sem"], 0) >= rec["val"]:
+            return
+        Q[q].wait_ge(T.sem[rec["sem"]], rec["val"])
+        for k, n in rec["snap"].items():
+            if clk[q].get(k, 0) < n:
+                clk[q][k] = n
+        clk[q][rec["sem"]] = rec["val"]
+
+    def issue(q, fn, reads, writes, sem=None, val=None, waw=True):
+        lab = q if sem is None else "dma"
+        deps = []
+        for kind, regs in (("r", reads), ("w", writes)):
+            for (nm, lo, hi) in regs:
+                ps = nm[:2] == "PB"
+                for rec in acc.get(nm, []):
+                    if not ps and (rec["hi"] <= lo or rec["lo"] >= hi):
+                        continue
+                    if rec["q"] == lab and lab != "dma":
+                        if q == "p" and ps:
+                            continue
+                        if kind == "r" and not rec["w"]:
+                            continue
+                        if kind == "w" and not waw:
+                            continue
+                        if ps and (rec["hi"] <= lo or rec["lo"] >= hi):
+                            continue
+                        deps.append(rec)
+                    elif rec["w"] or kind == "w" or ps:
+                        deps.append(rec)
+        deps.sort(key=lambda r: -r["idx"])
+        for rec in deps:
+            wait(q, rec)
+        ins = fn()
+        if sem is None:
+            CNT[q] += 1
+            ins.then_inc(T.sem["q" + q], 1)
+            s, n = "q" + q, CNT[q]
+        else:
+            s, n = sem, val
+            if ins is not None and val == 16:
+                ins.then_inc(T.sem[sem], 16)
+        snap = dict(clk[q])
+        idx[0] += 1
+        for w, regs in ((False, reads), (True, writes)):
+            for (nm, lo, hi) in regs:
+                old = acc.get(nm, [])
+                if w:
+                    old = [r for r in old if not (lo <= r["lo"] and r["hi"] <= hi)]
+                else:
+                    old = [r for r in old if r["w"] or not (r["q"] == lab and lab != "dma" and lo <= r["lo"] and r["hi"] <= hi)]
+                old.append({"lo": lo, "hi": hi, "w": w, "q": lab, "sem": s, "val": n, "snap": snap, "idx": idx[0]})
+                acc[nm] = old
+
+    def arrive(name, a, b, sem, val):
+        idx[0] += 1
+        acc.setdefault(name, []).append({"lo": a, "hi": b, "w": True, "q": "dma", "sem": sem, "val": val, "snap": {}, "idx": idx[0]})
+
+    def rd(*vs):
+        out = []
+        for v in vs:
+            if isinstance(v, tuple):
+                out += v[1]
+                if len(v) == 3:
+                    out += v[2]
+        return out
+
+    def ap(v):
+        return v[0] if isinstance(v, tuple) else v
+
+    def outs(o):
+        return o[1], (o[2] if len(o) == 3 else [])
+
+    def tt(o, a, b, op, waw=True):
+        w, r = outs(o)
+        issue("v", lambda: g.vector.tensor_tensor(ap(o), ap(a), ap(b), op), rd(a, b) + r, w, waw=waw)
+
+    def ts(o, a, s1, op0, s2=None, op1=None, waw=True):
+        def f():
+            if op1 is None:
+                return g.vector.tensor_scalar(ap(o), ap(a), ap(s1), None, op0)
+            return g.vector.tensor_scalar(ap(o), ap(a), ap(s1), ap(s2), op0, op1)
+        issue("v", f, rd(a, s1, s2), o[1], waw=waw)
+
+    def tc(o, a):
+        w, r = outs(o)
+        issue("v", lambda: g.vector.tensor_copy(ap(o), ap(a)), rd(a) + r, w)
+
+    def ms(o, c):
+        issue("v", lambda: g.vector.memset(ap(o), c), [], o[1], waw=True)
+
+    def scan(o, d0, d1, op0, op1):
+        issue("v", lambda: g.vector.tensor_tensor_scan(ap(o), ap(d0), ap(d1), 0.0, op0, op1), rd(d0, d1), o[1])
+
+    def red(o, a):
+        issue("v", lambda: g.vector.tensor_reduce(ap(o), ap(a), AxisListType.X, OP.add), rd(a), o[1])
+
+    def act(o, a, func, bias=0.0, scale=1.0):
+        issue("s", lambda: g.scalar.activation(ap(o), ap(a), func, bias=ap(bias), scale=scale), rd(a, bias), o[1])
+
+    def mm(o, l, r, start, stop):
+        issue("p", lambda: g.tensor.matmul(ap(o), ap(l), ap(r), start, stop), rd(l, r), o[1])
+
+    def iota(o, pat, base=0, cm=0):
+        def f():
+            if SCRATCH[o[1][0][0]][2] == "int32":
+                return g.iota(ap(o), pat, base, cm)
+            return g.iota(ap(o), pat, base, cm, allow_small_or_imprecise_dtypes=True)
+        issue("g", f, [], o[1])
+
+    def load(q, name, a, b, src, sem):
+        v = X(name, a, b)
+        issue(q, lambda: Q[q].dma_start(v[0], src), [], v[1], sem=sem, val=16)
+
+    def store(q, dst, v, sem):
+        issue(q, lambda: Q[q].dma_start(dst, v[0]), v[1], [], sem=sem, val=16)
+
+    def col(name, j):
+        return X(name, j, j + 1)
+
+    load("s", "Z0", 0, 256, T.sd[:, :], "dsd")
+    load("y", "V0", 0, 16, T.v0[:, :], "dv0")
+    load("y", "xt", 0, 4096, T.x[:, :], "dx")
+    load("s", "THI", 0, 4, T.th[:, :], "dth")
+
+    iota(X("PI"), [[0, 1]], 0, 1)
+    iota(X("GH"), [[8, 16], [0, 8]])
+    iota(X("IS"), [[0, 6], [1, 16]])
+    iota(X("TJ"), [[16, 8], [1, 2], [0, 8]])
+    iota(X("PQ"), [[-2, 8]], 0, 1)
+    iota(X("CJ"), [[1, 128]])
+    iota(X("GJ"), [[16, 8], [0, 16]])
+    iota(X("GM"), [[16, 8], [0, 2], [1, 8]])
+    iota(X("BE"), [[2, 8]])
+    iota(X("DPT", 0, 64), [[4, 64]], 256)
+    iota(X("DPT", 64, 128), [[8, 64]], 512)
+    iota(X("CLSR"), [[1, 4], [0, 64]])
+    iota(X("K96"), [[16, 6], [0, 16]], DUMP)
+
+    for m in range(8):
+        ms(col("KROW", m), float(KAP[m]))
+    ms(X("xt", 4096, 4224), 0.0)
+    ms(X("SEG"), 1.0)
+    ms(X("SEG", 0, 1024, 8), 0.0)
+    P, I16, M8, H2, G16 = [col("PC", j) for j in range(5)]
+    tc(col("PT", 0), X("PI"))
+    ts(col("PT", 1), X("PI"), 15, OP.bitwise_and)
+    ts(col("PT", 2), X("PI"), 7, OP.bitwise_and)
+    ts(col("PT", 3), X("PI"), 3, OP.logical_shift_right, 1, OP.bitwise_and)
+    ts(col("PT", 4), X("PI"), 112, OP.bitwise_and)
+    tc(X("PC"), X("PT"))
+    ts(col("DC", 0), G16, 8.0, OP.add)
+    ts(X("WU0"), X("GH"), G16, OP.is_equal)
+    ts(X("WU1"), X("GH"), col("DC", 0), OP.is_equal)
+    ts(X("KEQ"), X("IS", 0, 8), M8, OP.is_equal)
+    tt(X("KEQ"), X("KEQ"), X("KROW"), OP.mult)
+    red(col("KC", 0), X("KEQ"))
+    ts(col("KC", 1), col("KC", 0), 2.0, OP.mult)
+    tt(col("KC", 2), col("KC", 1), col("KC", 1), OP.mult)
+    ts(col("KC", 2), col("KC", 2), -1.0, OP.mult, -0.25, OP.add)
+    K2, KM = col("KC", 1), col("KC", 2)
+    for e in range(8):
+        ts(X("LP", 128 * e, 128 * e + 128), X("TJ"), col("PQ", e), OP.is_equal)
+    tc(X("VH0"), X("V0"))
+    tt(X("VL0"), X("V0"), X("VH0"), OP.subtract)
+
+    mm(X("PB0", 0, 128), X("WU0"), X("Z0", 0, 256, 2), True, False)
+    mm(X("PB0", 0, 128), X("WU1"), X("Z0", 1, 256, 2), False, True)
+    act(X("S0F"), X("PB0", 0, 128), AF.Square, bias=K2, scale=0.25)
+    act(X("CAT", 0, 128), X("PB0", 0, 128), AF.Copy)
+    for e in range(8):
+        mm(X("PB1", e, 128, 8), X("LP", 128 * e, 128 * e + 128), X("VH0"), True, False)
+        mm(X("PB1", e, 128, 8), X("LP", 128 * e, 128 * e + 128), X("VL0"), False, True)
+    ts(X("S0I"), X("S0F"), KM, OP.add)
+    tc(X("VCI"), X("PB1", 0, 128))
+    tt(X("TA"), X("S0I"), X("VCI"), OP.add)
+    ts(X("TR", 0, 128), X("TA"), 4095, OP.bitwise_and)
+    tc(X("LU", 0, 128), X("TR", 0, 128))
+    ts(X("ID"), X("CJ"), P, OP.is_equal)
+    ts(X("NI"), X("CJ"), P, OP.is_equal, -1.0, OP.mult)
+    tc(X("CAT", 256, 384), X("VCI"))
+    tc(X("THF"), X("THI"))
+
+    ts(X("BO"), X("GJ"), G16, OP.is_equal)
+    tt(col("DC", 1), G16, M8, OP.add)
+    ts(col("DC", 2), M8, 0.0, OP.is_equal)
+    tt(col("DC", 3), G16, H2, OP.add)
+    ts(col("DC", 4), H2, -1.0, OP.mult, 1.0, OP.add)
+    ts(col("DC", 5), H2, -1.0, OP.mult)
+    ts(col("DC", 6), col("DC", 2), col("DC", 4), OP.mult, 256.0, OP.mult)
+    ts(col("DC", 7), col("DC", 2), H2, OP.mult, 256.0, OP.mult)
+    ts(X("RK1"), X("GM"), col("DC", 1), OP.is_equal)
+    ts(X("RT1"), X("RK1"), col("DC", 5), OP.mult)
+    ts(X("RT2"), X("NI"), col("DC", 4), OP.mult)
+    tt(X("RK2"), X("RT1"), X("RT2"), OP.add)
+    ts(X("M1K"), X("NI"), 1024.0, OP.mult)
+    ts(X("N32"), X("NI"), 32.0, OP.mult)
+    ts(X("HS0"), X("BO"), col("DC", 6), OP.mult)
+    ts(X("HS1"), X("BO"), col("DC", 7), OP.mult)
+    ts(X("RI"), X("IS", 0, 16), I16, OP.is_equal)
+    ts(col("KC", 3), P, 0.0, OP.is_equal)
+    ts(X("E0"), X("CJ"), 0.0, OP.is_ge, col("KC", 3), OP.mult)
+    ts(X("KR1"), X("E0"), 1024.0, OP.mult)
+    ts(X("KR2"), X("E0"), 2097152.0, OP.mult)
+    ts(X("KR3"), X("E0"), 256.0, OP.mult)
+    ms(X("ONE"), 1.0)
+    ms(X("ZER"), 0.0)
+    ts(X("BE"), X("BE"), col("DC", 3), OP.add)
+    for e in range(8):
+        ts(X("PL", 128 * e, 128 * e + 128), X("CJ"), col("BE", e), OP.is_equal, col("DC", 2), OP.mult)
+    ts(col("ACOL", 1), H2, 2.0, OP.mult)
+    ts(col("ACOL", 2), H2, 4.0, OP.mult)
+    ts(X("DUMPP", 0, 64), X("DPT", 0, 64), col("ACOL", 1), OP.add)
+    ts(X("DUMPP", 64, 128), X("DPT", 64, 128), col("ACOL", 2), OP.add)
+    ms(X("XW", 0, 96), SENT)
+
+    def consts_verdict():
+        ts(X("DIAG"), X("IS"), I16, OP.is_equal)
+        ts(X("HOLD"), X("IS"), 0.0, OP.is_gt)
+        ts(X("OB"), X("DIAG"), -65536.0, OP.mult, 57344.0, OP.add)
+        ts(X("R0M"), X("IS"), 0.0, OP.is_equal)
+        ts(X("RST"), X("K96"), I16, OP.add)
+        tc(X("DMP6"), X("RST", 0, 96, 16))
+        tt(X("RST"), X("RST"), X("R0M"), OP.mult)
+        ts(X("BOK"), X("BO"), 8192.0, OP.mult)
+        for k in range(6):
+            ts(X("CODE", 16 * k, 16 * k + 16), X("DIAG", 16 * k, 16 * k + 16), float(16 ** k), OP.mult)
+            ms(col("W6", k), float(2 * 16 ** k))
+        ms(X("DN"), 0.0)
+        ms(X("FX", 900, 948, 4), 1.0)
+        ms(X("D"), 0.0)
+
+    def consts_back():
+        for i in range(16):
+            ts(X("RS", 128 * i, 128 * i + 128), X("BO"), col("RI", i), OP.mult)
+        ts(X("VS0"), X("WU0"), col("RI", 0), OP.mult)
+        ts(X("VS1"), X("WU1"), col("RI", 0), OP.mult)
+        ms(X("VWIN", 96, 1024), 0.0)
+
+    def consts_out():
+        for e in range(16):
+            ms(X("K8T", 16 * e, 16 * e + 16), float(8 * KAP[e % 8]))
+        tt(X("K2T"), X("K8T"), X("K8T"), OP.mult)
+        ts(X("K2T"), X("K2T"), -0.0625, OP.mult, -0.25, OP.add)
+        ms(X("YLI"), 0)
+        ts(X("YLI", 0, 8), X("YLI", 0, 8), I16, OP.add)
+        ts(X("YLI", 8, 16), X("YLI", 8, 16), I16, OP.add, 16.0, OP.add)
+        ts(X("YLI", 16, 32), X("YLI", 16, 32), I16, OP.add)
+        tc(X("YLU"), X("YLI"))
+
+    def gs(b, bt):
+        l0 = 128 * bt
+        c0 = 128 * b + l0 // 2
+        act(X("GT", 8 * l0, 8 * (l0 + NSC)), IND(X("xt"), X("LU", c0, c0 + NSC // 2)), AF.Copy)
+
+    def gv(b, bt):
+        l0 = 128 * bt + NSC
+        c0 = 128 * b + l0 // 2
+        tc(X("GT", 8 * l0, 8 * (l0 + NV)), IND(X("xt"), X("LU", c0, c0 + NV // 2)))
+
+    def smax(bt):
+        a = 1024 * bt
+        scan(X("HM", a, a + 1024), X("SEG"), X("GT", a, a + 1024), OP.mult, OP.max)
+
+    def diff(bt, zin):
+        l0 = 128 * bt
+        pb = "PB%d" % bt
+        mm(X(pb, 0, 128), X("NI"), X(zin, l0, l0 + 128), True, False)
+        mm(X(pb, 0, 128), X("ID"), X("HM", 8 * l0 + 7, 8 * l0 + 1024, 8), False, True)
+
+    def absz(bt, zout):
+        l0 = 128 * bt
+        act(X(zout, l0, l0 + 128), X("PB%d" % bt, 0, 128), AF.Abs)
+
+    def usum(bt):
+        l0, c0 = 128 * bt, 64 * bt
+        pb = "PB%d" % bt
+        mm(X(pb, 128, 192), X("WU0"), X("Z1", l0, l0 + 128, 2), True, False)
+        mm(X(pb, 128, 192), X("WU1"), X("Z1", l0 + 1, l0 + 128, 2), False, True)
+        act(X("SQ", c0, c0 + 64), X(pb, 128, 192), AF.Square, bias=K2, scale=0.25)
+        act(X("U1", c0, c0 + 64), X(pb, 128, 192), AF.Copy)
+
+    def list1(bt):
+        c0 = 64 * bt
+        tt(X("T1", c0, c0 + 64), X("SQ", c0, c0 + 64), X("VM", c0, c0 + 64), OP.add)
+        ts(X("TR", 128 + c0, 192 + c0), X("T1", c0, c0 + 64), 4095, OP.bitwise_and)
+        tc(X("LU", 128 + c0, 192 + c0), X("TR", 128 + c0, 192 + c0))
+
+    def vsplit():
+        ts(X("VM"), X("VCI"), KM, OP.add)
+        tc(X("VHI"), X("VCI"))
+        tt(X("VLO"), X("VCI"), X("VHI"), OP.subtract)
+
+    def newv():
+        ts(X("TA"), X("WI"), col("ACOL", 0), OP.add)
+        ts(X("VCI"), X("TA"), 4095, OP.bitwise_and)
+
+    def hurt():
+        tt(X("FX", 960, 966), X("DN", 0, 6), X("W6"), OP.mult)
+        red(col("FX", 966), X("FX", 960, 966))
+        ts(col("FX", 967), col("FX", 966), float(0x111111), OP.add)
+        ts(X("MS", 0, 256), X("N3", 512, 768), col("FX", 967), OP.add)
+        ts(X("MS", 256, 512), X("MS", 0, 256), 0x444444, OP.bitwise_and)
+        ts(X("HB"), X("MS", 256, 512), 0.0, OP.is_gt)
+
+    def back(t):
+        arrive("RR", 8 * t, 8 * t + 8, "rin%d" % t, NE)
+        for i in range(16):
+            mm(X("PB7", i, 96, 16), X("RS", 128 * i, 128 * i + 128), X("RR", 8 * t, 8 * t + 6), True, True)
+        act(X("VWIN", 0, 96), X("PB7", 0, 96), AF.Copy, bias=1.0, scale=-1.0)
+        act(X("VROW"), IND(X("VWIN"), X("OL")), AF.Copy)
+
+    def thaw():
+        mm(X("PB7", 128, 256), X("VS0"), X("VROW", 0, 256, 2), True, False)
+        mm(X("PB7", 128, 256), X("VS1"), X("VROW", 1, 256, 2), False, False)
+        for cl in range(4):
+            for h in range(2):
+                mm(X("PB7", 128 + 32 * cl, 160 + 32 * cl), X("WU%d" % h), X("HB", 4 * h + cl, 256, 8), False, cl + h == 4)
+        tt(X("FR"), X("PB7", 128, 256), X("NF2"), OP.is_equal)
+
+    V = X("CAT", 256, 384)
+    S6 = X("FX", 207, 288, 16)
+
+    for t in range(STAGES):
+        dst = T.cores[_partner(rank, t)]
+        hop = dst if topo.may_write(core, dst) else _relay(core, T, topo)
+        if t:
+            ts(X("TA"), X("ZN"), col("ACOL", 0), OP.add)
+            ts(X("TR", 0, 128), X("TA"), 4095, OP.bitwise_and)
+            tc(X("LU", 0, 128), X("TR", 0, 128))
+            tt(X("FX", 972, 978), X("DN", 0, 6), X("FX", 980, 986), OP.mult)
+            tt(X("FX", 972, 978), X("FX", 972, 978), X("DMP6"), OP.add)
+            ts(X("DLU", 6, 12), X("FX", 972, 978), -1.0, OP.add)
+            tc(IND(X("xt"), X("DLU", 6, 12)), X("N3", 896, 992))
+        gs(0, 0)
+        gv(0, 0)
+        gs(0, 1)
+        if t:
+            newv()
+        vsplit()
+        mm(X("PB3", 0, 256), X("KR2"), X("CLSR"), True, False)
+        mm(X("PB3", 0, 256), X("KR3"), X("ONE"), False, False)
+        for h in range(2):
+            mm(X("PB3", h, 256, 2), X("HS%d" % h), X("VHI"), False, False)
+            mm(X("PB3", h, 256, 2), X("HS%d" % h), X("VLO"), False, False)
+        smax(0)
+        diff(0, "Z0")
+        absz(0, "Z1")
+        usum(0)
+        gv(0, 1)
+        if t:
+            hurt()
+        smax(1)
+        diff(1, "Z0")
+        absz(1, "Z1")
+        usum(1)
+        list1(0)
+        gs(1, 0)
+        gv(1, 0)
+        list1(1)
+        gs(1, 1)
+        smax(0)
+        diff(0, "Z1")
+        gv(1, 1)
+        absz(0, "Z2")
+        ts(X("GE", 0, 128), X("Z2", 0, 128), col("THF", t), OP.is_ge)
+        if t:
+            back(t - 1)
+        smax(1)
+        diff(1, "Z1")
+        absz(1, "Z2")
+        ts(X("GE", 128, 256), X("Z2", 128, 256), col("THF", t), OP.is_ge)
+        if t:
+            thaw()
+        mm(X("PB2", 0, 128), X("WU0"), X("GE", 0, 256, 2), True, False)
+        mm(X("PB2", 0, 128), X("WU1"), X("GE", 1, 256, 2), False, not t)
+        if t:
+            mm(X("PB2", 0, 128), X("N32"), X("FR"), False, True)
+        mm(X("PB3", 0, 128), X("ID"), X("Z2", 0, 128), False, False)
+        mm(X("PB3", 128, 256), X("ID"), X("Z2", 128, 256), False, True)
+        act(X("XF"), X("PB3", 0, 256), AF.Copy)
+        ts(X("FL"), X("PB2", 0, 128), 8.5, OP.is_ge)
+        scan(X("INC"), X("FL"), X("ZER"), OP.add, OP.add)
+        mm(X("PB2", 128, 256), X("KR1"), X("ONE", 0, 128), True, False)
+        mm(X("PB2", 128, 256), X("RK2"), X("FL"), False, False)
+        mm(X("PB2", 128, 256), X("M1K"), X("FL"), False, False)
+        mm(X("PB2", 128, 256), X("RK1"), X("INC"), False, True)
+        tt(X("OFFP"), X("PB2", 128, 256), X("DUMPP"), OP.min)
+        for e in range(8):
+            mm(X("PB2", 256, 272), X("PL", 128 * e, 128 * e + 128), X("OFFP", e, 128, 8), e == 0, e == 7)
+        tc(X("OL"), X("PB2", 256, 272))
+        tc(IND(X("XW"), X("OL")), X("XF"))
+        sv = X("XW", 0, 96)
+        issue("g", lambda: _send(g, T, topo, core, hop, T.XR[:, 96 * t:96 * t + 96], sv[0], "xin%d" % t, "xl%d" % t),
+              sv[1], [], sem="xl%d" % t, val=NE)
+        if t == 0:
+            consts_verdict()
+        ts(X("GO"), X("OFFP"), 95.5, OP.is_lt)
+        ts(X("P1"), X("TR"), 1.0, OP.add)
+        if t == 0:
+            for b in range(2):
+                tt(X("LG", 128 * b, 128 * b + 128), X("P1", 128 * b, 128 * b + 128), X("GO"), OP.mult)
+            ts(X("NF2"), X("GO"), -1.0, OP.add)
+        else:
+            for b in range(2):
+                tt(X("P1", 128 * b, 128 * b + 128), X("P1", 128 * b, 128 * b + 128), X("GO"), OP.mult)
+                tt(X("LG", 128 * b, 128 * b + 128), X("LG", 128 * b, 128 * b + 128), X("FR"), OP.mult)
+            tt(X("LG"), X("LG"), X("P1"), OP.add)
+            tt(X("NF2"), X("FR"), X("GO"), OP.add)
+            ts(X("NF2"), X("NF2"), -1.0, OP.add)
+        tc(X("LGU"), X("LG"))
+        if t:
+            tc(IND(X("D"), X("DLU", 0, 6)), X("ZER", 0, 96))
+            tt(X("SEL", 0, 128), V, X("VCI"), OP.subtract)
+            tt(X("SEL", 0, 128), X("SEL", 0, 128), X("FR"), OP.mult)
+            tt(V, X("SEL", 0, 128), X("VCI"), OP.add)
+            tt(X("SEL", 128, 256), X("CAT", 128, 256), X("U1"), OP.subtract)
+            tt(X("SEL", 128, 256), X("SEL", 128, 256), X("FR"), OP.mult)
+            tt(X("CAT", 128, 256), X("SEL", 128, 256), X("U1"), OP.add)
+        else:
+            act(X("CAT", 128, 256), X("U1"), AF.Copy)
+        act(X("WT", 0, 128), V, AF.Square)
+        act(X("WT", 128, 256), V, AF.Copy, scale=37.0)
+        act(X("WT", 0, 128), X("WT", 0, 128), AF.Copy, bias=-0.25, scale=0.125)
+        tt(X("WI"), X("WT", 0, 128), X("WT", 128, 256), OP.add)
+        if t < STAGES - 1:
+            tt(X("ZS"), X("WI"), X("S0I"), OP.add)
+            ts(X("ZN"), X("ZS"), 4095, OP.bitwise_and)
+            ms(X("XW", 0, 96), SENT)
+        if t == 0:
+            consts_back()
+            consts_out()
+        if t == STAGES - 1:
+            tc(X("CH"), X("CAT"))
+            tt(X("CL"), X("CAT"), X("CH"), OP.subtract)
+            for e in range(8):
+                mm(X("PB6", 256, 304), X("PL", 128 * e, 128 * e + 128), X("CH", e, 384, 8), e == 0, False)
+                mm(X("PB6", 256, 304), X("PL", 128 * e, 128 * e + 128), X("CL", e, 384, 8), False, e == 7)
+            tc(X("UL"), X("PB6", 256, 304))
+            tt(X("FX", 288, 544), IND(X("UL", 0, 32), X("YLU", 0, 16)), X("K8T"), OP.add)
+            act(X("FX", 544, 800), X("FX", 288, 544), AF.Square, scale=0.25)
+            tt(X("FX", 288, 544), X("FX", 544, 800), X("K2T"), OP.add)
+            tt(X("MS", 0, 256), IND(X("UL", 32, 48), X("YLU", 16, 32)), X("FX", 288, 544), OP.add)
+            ts(X("MS", 256, 512), X("MS", 0, 256), 4095, OP.bitwise_and)
+            tc(X("YO"), X("MS", 256, 512))
+            store("y", T.yt[:, :], X("YO"), "dyt")
+        arrive("XR", 96 * t, 96 * t + 96, "xin%d" % t, NE)
+        XR = X("XR", 96 * t, 96 * t + 96)
+        Y1 = X("N3", 800, 896)
+        ts(Y1, XR, 8, OP.logical_shift_right, 8191, OP.bitwise_and)
+        tt(X("FX", 0, 96), Y1, X("DIAG"), OP.mult)
+        scan(X("FX", 96, 192), X("HOLD"), X("FX", 0, 96), OP.mult, OP.add)
+        pos = []
+        o = 96
+        for k in range(5):
+            n = 80 - 16 * k
+            ts(X("E", o, o + n), X("N3", 816 + 16 * k, 896), col("FX", 96 + 16 * k + 15), OP.is_equal)
+            pos.append((o, n))
+            o += n
+        tt(X("E", 0, 96), Y1, X("FX", 96, 192), OP.is_equal)
+        mm(X("PB4", 0, 96), X("ID"), X("OB"), True, False)
+        for (o, n) in pos:
+            mm(X("PB4", 96 - n, 96), X("BOK"), X("E", o, o + n), False, False)
+        mm(X("PB4", 0, 96), X("BOK"), X("E", 0, 96), False, True)
+        tt(X("FX", 0, 96), X("PB4", 0, 96), Y1, OP.add)
+        scan(X("FX", 192, 288), X("RST"), X("FX", 0, 96), OP.max, OP.min)
+        tc(X("DLU", 0, 6), S6)
+        tc(IND(X("D"), X("DLU", 0, 6)), X("CODE"))
+        A = 96
+        for b in range(2):
+            c0, q0 = 128 * b, 2048 * b
+            tc(X("G2", q0, q0 + 8 * A), IND(X("D"), X("LGU", c0, c0 + A // 2)))
+            cuts = [A, 256] if b == 0 else [A, 192, 256]
+            for p in range(len(cuts) - 1):
+                act(X("G2", q0 + 8 * cuts[p], q0 + 8 * cuts[p + 1]), IND(X("D"), X("LGU", c0 + cuts[p] // 2, c0 + cuts[p + 1] // 2)), AF.Copy)
+            for p0, p1 in zip([0] + cuts[:-1], cuts):
+                for l0 in range(64 * (p0 // 64), p1, 64):
+                    a0, a1, cl = max(l0, p0), min(l0 + 64, p1), l0 // 64
+                    for m in range(8):
+                        mm(X("PB%d" % (5 + b), 4 * (a0 - l0) + cl, 4 * (a1 - l0), 4), X("ID"), X("G2", q0 + 8 * a0 + m, q0 + 8 * a1, 8), m == 0, m == 7)
+        ts(X("MS", 0, 96), XR, 21, OP.logical_shift_right)
+        tt(X("FX", 0, 96), X("MS", 0, 96), X("DIAG"), OP.mult)
+        scan(X("FX", 96, 192), X("HOLD"), X("FX", 0, 96), OP.mult, OP.add)
+        for cl in range(1, 4):
+            for p in (0, 4):
+                ts(X("FX", 900 + p + cl, 948, 8), X("FX", 111, 192, 16), float(cl), OP.is_ge, waw=False)
+        ts(X("FX", 990, 996), S6, 4100.0, OP.is_ge, -1.0, OP.mult)
+        tt(X("FX", 980, 986), S6, X("DMP6"), OP.subtract)
+        ts(X("N3", 896, 992), XR, 255, OP.bitwise_and)
+        for b in range(2):
+            ts(X("MS", 256 * b, 256 * b + 256), X("PB%d" % (5 + b), 0, 256), float(0x777777), OP.add)
+            ts(X("N3", 256 * b, 256 * b + 256), X("MS", 256 * b, 256 * b + 256), 0x888888, OP.bitwise_and, 3, OP.logical_shift_right)
+        tt(X("N3", 512, 768), X("N3", 0, 256), X("N3", 256, 512), OP.add)
+        tt(X("MS", 0, 128), X("N3", 512, 640), X("N3", 640, 768), OP.add)
+        tt(X("MS", 128, 192), X("MS", 0, 64), X("MS", 64, 128), OP.add)
+        ts(X("MS", 192, 256), X("MS", 128, 192), float(0x777777), OP.add)
+        ts(X("MS", 256, 320), X("MS", 192, 256), 0x888888, OP.bitwise_and, 3, OP.logical_shift_right)
+        tt(X("MS", 320, 352), X("MS", 256, 288), X("MS", 288, 320), OP.add)
+        tt(X("MS", 352, 368), X("MS", 320, 336), X("MS", 336, 352), OP.add)
+        tt(X("MS", 368, 376), X("MS", 352, 360), X("MS", 360, 368), OP.add)
+        for k in range(6):
+            ts(X("MS", 384 + 8 * k, 392 + 8 * k), X("MS", 368, 376), 4 * k, OP.logical_shift_right, 15, OP.bitwise_and)
+        tt(X("FX", 1000, 1048), X("MS", 384, 432), X("FX", 900, 948), OP.mult)
+        tt(X("FX", 1048, 1072), X("FX", 1000, 1048, 2), X("FX", 1001, 1048, 2), OP.add)
+        tt(X("FX", 1072, 1084), X("FX", 1048, 1072, 2), X("FX", 1049, 1072, 2), OP.add)
+        tt(X("FX", 1060, 1066), X("FX", 1072, 1084, 2), X("FX", 1073, 1084, 2), OP.add)
+        tt(X("DN", 0, 6), X("FX", 1060, 1066), X("FX", 990, 996), OP.is_equal)
+        dv = X("DN", 0, 8)
+        issue("g", lambda: _send(g, T, topo, core, hop, T.RR[:, 8 * t:8 * t + 8], dv[0], "rin%d" % t, "rl%d" % t),
+              dv[1], [], sem="rl%d" % t, val=NE)
+        mm(X("PB4", 128, 134), X("ONE", 0, 128), X("DN", 0, 6), True, True)
+        red(col("ACOL", 0), X("PB4", 128, 134))
+
+    newv()
+    tc(X("VHI"), X("VCI"))
+    tt(X("VLO"), X("VCI"), X("VHI"), OP.subtract)
+    for e in range(8):
+        mm(X("PB3", 0, 16), X("PL", 128 * e, 128 * e + 128), X("VHI", e, 128, 8), e == 0, False)
+        mm(X("PB3", 0, 16), X("PL", 128 * e, 128 * e + 128), X("VLO", e, 128, 8), False, e == 7)
+    hurt()
+    tc(X("FIN", 0, 16), X("PB3", 0, 16))
+    tt(X("FIN", 16, 32), X("UL", 32, 48), X("FIN", 0, 16), OP.subtract)
+    back(STAGES - 1)
+    thaw()
+    for e in range(8):
+        mm(X("PB2", 0, 16), X("PL", 128 * e, 128 * e + 128), X("FR", e, 128, 8), e == 0, e == 7)
+    tc(X("YS", 16, 32), X("PB2", 0, 16))
+    tt(X("FIN", 32, 48), X("FIN", 16, 32), X("YS", 16, 32), OP.mult)
+    tt(X("YS", 0, 16), X("FIN", 32, 48), X("FIN", 0, 16), OP.add)
+    store("y", T.ys[:, :], X("YS"), "dys")
+
+    for n, v in [("dx", 16), ("dsd", 16), ("dv0", 16), ("dth", 16), ("dyt", 16), ("dys", 16)]:
+        g.wait_ge(T.sem[n], v)
+    for q in "vspg":
+        g.wait_ge(T.sem["q" + q], CNT[q])
+    for t in range(STAGES):
+        for n in ("xin", "rin", "xl", "rl"):
+            g.wait_ge(T.sem[n + str(t)], NE)

@@ -5,7 +5,7 @@ KAP = (3, 29, 71, 113, 151, 197, 233, 277)
 STAGES, CAP = 4, 96
 NE = 8
 DUMP = 4112
-NV, NSC = 48, 80
+NV, NSC = 40, 88
 SENT = 8191 * 256
 
 _F, _B, _I, _U = "float32", "bfloat16", "int32", "uint16"
@@ -17,16 +17,16 @@ def _sb(n, d):
 
 SCRATCH = {
     "xt": _sb(4224, _B), "D": _sb(4224, _B), "Z0": _sb(256, _B), "Z1": _sb(256, _B), "Z2": _sb(256, _B),
-    "V0": _sb(16, _I), "THI": _sb(4, _I), "THF": _sb(4, _F),
+    "V0": _sb(16, _I), "THI": _sb(4, _I), "NTH": _sb(4, _F),
     "GT": _sb(2048, _B), "HM": _sb(2048, _B), "SEG": _sb(1024, _B), "G2": _sb(4096, _B),
     "CJ": _sb(128, _F), "GJ": _sb(128, _F), "GH": _sb(128, _F), "GM": _sb(128, _F), "TJ": _sb(128, _F),
     "IS": _sb(96, _F), "K96": _sb(96, _F), "PI": _sb(1, _I), "PT": _sb(5, _I), "PC": _sb(5, _F), "DC": _sb(8, _F),
     "BE": _sb(8, _F), "PQ": _sb(8, _F), "KROW": _sb(8, _F), "KEQ": _sb(8, _F), "KC": _sb(4, _F), "RI": _sb(16, _F),
     "CLSR": _sb(256, _B), "DUMPP": _sb(128, _F), "DPT": _sb(128, _F),
     "BO": _sb(128, _B), "BOK": _sb(128, _B), "WU0": _sb(128, _B), "WU1": _sb(128, _B), "ID": _sb(128, _B), "NI": _sb(128, _B),
-    "N32": _sb(128, _B), "M1K": _sb(128, _B), "RK1": _sb(128, _B), "RK2": _sb(128, _B), "RT1": _sb(128, _B), "RT2": _sb(128, _B),
+    "NF4": _sb(128, _B), "M1K": _sb(128, _B), "RK1": _sb(128, _B), "RK2": _sb(128, _B), "RT1": _sb(128, _B), "RT2": _sb(128, _B),
     "PL": _sb(1024, _B), "LP": _sb(1024, _B), "HS0": _sb(128, _B), "HS1": _sb(128, _B), "RS": _sb(2048, _B),
-    "VS0": _sb(128, _B), "VS1": _sb(128, _B), "E0": _sb(128, _B), "KR1": _sb(128, _B), "KR2": _sb(128, _B), "KR3": _sb(128, _B),
+    "VS0": _sb(128, _B), "VS1": _sb(128, _B), "FLX": _sb(128, _B), "KR1": _sb(128, _B), "KR2": _sb(128, _B), "KR3": _sb(128, _B),
     "ONE": _sb(256, _B), "ZER": _sb(128, _B), "DIAG": _sb(96, _F), "HOLD": _sb(96, _F), "RST": _sb(96, _F), "OB": _sb(96, _B),
     "R0M": _sb(96, _F), "CODE": _sb(96, _B), "DMP6": _sb(6, _F), "W6": _sb(6, _F), "K8T": _sb(256, _F), "K2T": _sb(256, _F),
     "YLI": _sb(32, _I), "YLU": _sb(32, _U),
@@ -37,7 +37,7 @@ SCRATCH = {
     "OL": _sb(16, _U), "XF": _sb(256, _F), "XW": _sb(1024, _I), "GO": _sb(128, _B), "FR": _sb(128, _B), "NF2": _sb(128, _B),
     "P1": _sb(256, _I), "LG": _sb(256, _I), "LGU": _sb(256, _U), "WT": _sb(384, _F), "WI": _sb(128, _I), "ZS": _sb(128, _I),
     "ZN": _sb(128, _I), "SEL": _sb(256, _F),
-    "XR": _sb(384, _I), "RR": _sb(32, _B), "MS": _sb(512, _I), "VWIN": _sb(1024, _B),
+    "XR": _sb(384, _I), "VO": _sb(96, _B), "MS": _sb(512, _I), "VWIN": _sb(1024, _B),
     "E": _sb(336, _B), "FX": _sb(1152, _F), "N3": _sb(1024, _I), "DLU": _sb(12, _U), "DN": _sb(8, _B), "HB": _sb(256, _B),
     "VROW": _sb(256, _B), "ACOL": _sb(4, _F), "UL": _sb(48, _F), "YO": _sb(256, _F), "YS": _sb(32, _F), "FIN": _sb(96, _F),
 }
@@ -81,7 +81,7 @@ def _relay_program(g, core, T, topo, c):
         g.wait_ge(T.sem["xin%d" % t], NE)
         _send(g, T, topo, core, d, T.XR[:, 96 * t:96 * t + 96], T.XR[:, 96 * t:96 * t + 96], "xin%d" % t, "xl%d" % t)
         g.wait_ge(T.sem["rin%d" % t], NE)
-        _send(g, T, topo, core, d, T.RR[:, 8 * t:8 * t + 8], T.RR[:, 8 * t:8 * t + 8], "rin%d" % t, "rl%d" % t)
+        _send(g, T, topo, core, d, T.VWIN[:, 0:96], T.G2[:, 96 * t:96 * t + 96], "rin%d" % t, "rl%d" % t)
         used.append(t)
     for t in used:
         g.wait_ge(T.sem["xl%d" % t], NE)
@@ -208,7 +208,7 @@ def rank_program(g, core, T, topo):
         issue("v", lambda: g.vector.tensor_reduce(ap(o), ap(a), AxisListType.X, OP.add), rd(a), o[1])
 
     def act(o, a, func, bias=0.0, scale=1.0):
-        issue("s", lambda: g.scalar.activation(ap(o), ap(a), func, bias=ap(bias), scale=scale), rd(a, bias), o[1])
+        issue("s", lambda: g.scalar.activation(ap(o), ap(a), func, bias=ap(bias), scale=ap(scale)), rd(a, bias, scale), o[1])
 
     def mm(o, l, r, start, stop):
         issue("p", lambda: g.tensor.matmul(ap(o), ap(l), ap(r), start, stop), rd(l, r), o[1])
@@ -248,12 +248,13 @@ def rank_program(g, core, T, topo):
     iota(X("DPT", 64, 128), [[8, 64]], 512)
     iota(X("CLSR"), [[1, 4], [0, 64]])
     iota(X("K96"), [[16, 6], [0, 16]], DUMP)
+    iota(X("HM", 0, 1024), [[0, 128], [1, 8]])
+    iota(X("VWIN", 96, 1024), [[0, 928]])
+    iota(X("D"), [[0, 4224]])
 
     for m in range(8):
         ms(col("KROW", m), float(KAP[m]))
     ms(X("xt", 4096, 4224), 0.0)
-    ms(X("SEG"), 1.0)
-    ms(X("SEG", 0, 1024, 8), 0.0)
     P, I16, M8, H2, G16 = [col("PC", j) for j in range(5)]
     tc(col("PT", 0), X("PI"))
     ts(col("PT", 1), X("PI"), 15, OP.bitwise_and)
@@ -280,6 +281,7 @@ def rank_program(g, core, T, topo):
     mm(X("PB0", 0, 128), X("WU1"), X("Z0", 1, 256, 2), False, True)
     act(X("S0F"), X("PB0", 0, 128), AF.Square, bias=K2, scale=0.25)
     act(X("CAT", 0, 128), X("PB0", 0, 128), AF.Copy)
+    act(X("SEG"), X("HM", 0, 1024), AF.Sign)
     for e in range(8):
         mm(X("PB1", e, 128, 8), X("LP", 128 * e, 128 * e + 128), X("VH0"), True, False)
         mm(X("PB1", e, 128, 8), X("LP", 128 * e, 128 * e + 128), X("VL0"), False, True)
@@ -291,7 +293,7 @@ def rank_program(g, core, T, topo):
     ts(X("ID"), X("CJ"), P, OP.is_equal)
     ts(X("NI"), X("CJ"), P, OP.is_equal, -1.0, OP.mult)
     tc(X("CAT", 256, 384), X("VCI"))
-    tc(X("THF"), X("THI"))
+    ts(X("NTH"), X("THI"), -1.0, OP.mult, 0.5, OP.add)
 
     ts(X("BO"), X("GJ"), G16, OP.is_equal)
     tt(col("DC", 1), G16, M8, OP.add)
@@ -302,19 +304,15 @@ def rank_program(g, core, T, topo):
     ts(col("DC", 6), col("DC", 2), col("DC", 4), OP.mult, 256.0, OP.mult)
     ts(col("DC", 7), col("DC", 2), H2, OP.mult, 256.0, OP.mult)
     ts(X("RK1"), X("GM"), col("DC", 1), OP.is_equal)
-    ts(X("RT1"), X("RK1"), col("DC", 5), OP.mult)
-    ts(X("RT2"), X("NI"), col("DC", 4), OP.mult)
-    tt(X("RK2"), X("RT1"), X("RT2"), OP.add)
-    ts(X("M1K"), X("NI"), 1024.0, OP.mult)
-    ts(X("N32"), X("NI"), 32.0, OP.mult)
-    ts(X("HS0"), X("BO"), col("DC", 6), OP.mult)
-    ts(X("HS1"), X("BO"), col("DC", 7), OP.mult)
+    act(X("RT1"), X("RK1"), AF.Identity, scale=col("DC", 5))
+    act(X("RT2"), X("NI"), AF.Identity, scale=col("DC", 4))
+    act(X("M1K"), X("NI"), AF.Copy, scale=1024.0)
+    act(X("HS0"), X("BO"), AF.Identity, scale=col("DC", 6))
+    act(X("HS1"), X("BO"), AF.Identity, scale=col("DC", 7))
     ts(X("RI"), X("IS", 0, 16), I16, OP.is_equal)
-    ts(col("KC", 3), P, 0.0, OP.is_equal)
-    ts(X("E0"), X("CJ"), 0.0, OP.is_ge, col("KC", 3), OP.mult)
-    ts(X("KR1"), X("E0"), 1024.0, OP.mult)
-    ts(X("KR2"), X("E0"), 2097152.0, OP.mult)
-    ts(X("KR3"), X("E0"), 256.0, OP.mult)
+    ms(X("KR1"), 8.0)
+    ms(X("KR2"), 16384.0)
+    ms(X("KR3"), 2.0)
     ms(X("ONE"), 1.0)
     ms(X("ZER"), 0.0)
     ts(X("BE"), X("BE"), col("DC", 3), OP.add)
@@ -325,35 +323,33 @@ def rank_program(g, core, T, topo):
     ts(X("DUMPP", 0, 64), X("DPT", 0, 64), col("ACOL", 1), OP.add)
     ts(X("DUMPP", 64, 128), X("DPT", 64, 128), col("ACOL", 2), OP.add)
     ms(X("XW", 0, 96), SENT)
+    tt(X("RK2"), X("RT1"), X("RT2"), OP.add)
 
     def consts_verdict():
         ts(X("DIAG"), X("IS"), I16, OP.is_equal)
         ts(X("HOLD"), X("IS"), 0.0, OP.is_gt)
-        ts(X("OB"), X("DIAG"), -65536.0, OP.mult, 57344.0, OP.add)
+        act(X("OB"), X("DIAG"), AF.Copy, bias=57344.0, scale=-65536.0)
+        act(X("BOK"), X("BO"), AF.Copy, scale=8192.0)
         ts(X("R0M"), X("IS"), 0.0, OP.is_equal)
         ts(X("RST"), X("K96"), I16, OP.add)
         tc(X("DMP6"), X("RST", 0, 96, 16))
         tt(X("RST"), X("RST"), X("R0M"), OP.mult)
-        ts(X("BOK"), X("BO"), 8192.0, OP.mult)
         for k in range(6):
-            ts(X("CODE", 16 * k, 16 * k + 16), X("DIAG", 16 * k, 16 * k + 16), float(16 ** k), OP.mult)
+            act(X("CODE", 16 * k, 16 * k + 16), X("DIAG", 16 * k, 16 * k + 16), AF.Copy, scale=float(16 ** k))
             ms(col("W6", k), float(2 * 16 ** k))
-        ms(X("DN"), 0.0)
-        ms(X("FX", 900, 948, 4), 1.0)
-        ms(X("D"), 0.0)
+        ms(X("FX", 900, 948, 4), 8192.0)
 
     def consts_back():
         for i in range(16):
-            ts(X("RS", 128 * i, 128 * i + 128), X("BO"), col("RI", i), OP.mult)
-        ts(X("VS0"), X("WU0"), col("RI", 0), OP.mult)
-        ts(X("VS1"), X("WU1"), col("RI", 0), OP.mult)
-        ms(X("VWIN", 96, 1024), 0.0)
+            act(X("RS", 128 * i, 128 * i + 128), X("BO"), AF.Identity, scale=col("RI", i))
+        act(X("VS0"), X("WU0"), AF.Identity, scale=col("RI", 0))
+        act(X("VS1"), X("WU1"), AF.Identity, scale=col("RI", 0))
 
     def consts_out():
         for e in range(16):
-            ms(X("K8T", 16 * e, 16 * e + 16), float(8 * KAP[e % 8]))
-        tt(X("K2T"), X("K8T"), X("K8T"), OP.mult)
-        ts(X("K2T"), X("K2T"), -0.0625, OP.mult, -0.25, OP.add)
+            act(X("K8T", 16 * e, 16 * e + 16), X("IS", 0, 16), AF.Copy, bias=float(8 * KAP[e % 8]), scale=0.0)
+        act(X("K2T"), X("K8T"), AF.Square, scale=0.25)
+        act(X("K2T"), X("K2T"), AF.Copy, bias=-0.25, scale=-1.0)
         ms(X("YLI"), 0)
         ts(X("YLI", 0, 8), X("YLI", 0, 8), I16, OP.add)
         ts(X("YLI", 8, 16), X("YLI", 8, 16), I16, OP.add, 16.0, OP.add)
@@ -398,37 +394,45 @@ def rank_program(g, core, T, topo):
         ts(X("TR", 128 + c0, 192 + c0), X("T1", c0, c0 + 64), 4095, OP.bitwise_and)
         tc(X("LU", 128 + c0, 192 + c0), X("TR", 128 + c0, 192 + c0))
 
-    def vsplit():
-        ts(X("VM"), X("VCI"), KM, OP.add)
-        tc(X("VHI"), X("VCI"))
-        tt(X("VLO"), X("VCI"), X("VHI"), OP.subtract)
-
     def newv():
         ts(X("TA"), X("WI"), col("ACOL", 0), OP.add)
         ts(X("VCI"), X("TA"), 4095, OP.bitwise_and)
 
-    def hurt():
-        tt(X("FX", 960, 966), X("DN", 0, 6), X("W6"), OP.mult)
-        red(col("FX", 966), X("FX", 960, 966))
-        ts(col("FX", 967), col("FX", 966), float(0x111111), OP.add)
-        ts(X("MS", 0, 256), X("N3", 512, 768), col("FX", 967), OP.add)
-        ts(X("MS", 256, 512), X("MS", 0, 256), 0x444444, OP.bitwise_and)
-        ts(X("HB"), X("MS", 256, 512), 0.0, OP.is_gt)
+    def hurt(step):
+        if step == 0:
+            tt(X("FX", 960, 966), X("DN", 0, 6), X("W6"), OP.mult)
+        elif step == 1:
+            red(col("FX", 966), X("FX", 960, 966))
+        elif step == 2:
+            ts(col("FX", 967), col("FX", 966), float(0x111111), OP.add)
+        elif step == 3:
+            ts(X("MS", 0, 256), X("N3", 512, 768), col("FX", 967), OP.add)
+        elif step == 4:
+            ts(X("MS", 256, 512), X("MS", 0, 256), 0x444444, OP.bitwise_and)
+        else:
+            ts(X("HB"), X("MS", 256, 512), 0.0, OP.is_gt)
 
     def back(t):
-        arrive("RR", 8 * t, 8 * t + 8, "rin%d" % t, NE)
-        for i in range(16):
-            mm(X("PB7", i, 96, 16), X("RS", 128 * i, 128 * i + 128), X("RR", 8 * t, 8 * t + 6), True, True)
-        act(X("VWIN", 0, 96), X("PB7", 0, 96), AF.Copy, bias=1.0, scale=-1.0)
+        arrive("VWIN", 0, 96, "rin%d" % t, NE)
         act(X("VROW"), IND(X("VWIN"), X("OL")), AF.Copy)
 
-    def thaw():
-        mm(X("PB7", 128, 256), X("VS0"), X("VROW", 0, 256, 2), True, False)
-        mm(X("PB7", 128, 256), X("VS1"), X("VROW", 1, 256, 2), False, False)
+    def thaw1():
+        mm(X("PB7", 128, 256), X("ID"), X("NF2"), True, False)
         for cl in range(4):
             for h in range(2):
-                mm(X("PB7", 128 + 32 * cl, 160 + 32 * cl), X("WU%d" % h), X("HB", 4 * h + cl, 256, 8), False, cl + h == 4)
-        tt(X("FR"), X("PB7", 128, 256), X("NF2"), OP.is_equal)
+                mm(X("PB7", 128 + 32 * cl, 160 + 32 * cl), X("WU%d" % h), X("HB", 4 * h + cl, 256, 8), False, False)
+
+    def thaw2():
+        mm(X("PB7", 128, 256), X("VS0"), X("VROW", 0, 256, 2), False, False)
+        mm(X("PB7", 128, 256), X("VS1"), X("VROW", 1, 256, 2), False, True)
+
+    def verdict_row(t, hop):
+        for i in range(16):
+            mm(X("PB7", i, 96, 16), X("RS", 128 * i, 128 * i + 128), X("DN", 0, 6), True, True)
+        act(X("VO"), X("PB7", 0, 96), AF.Copy, bias=1.0, scale=-1.0)
+        out = T.VWIN[:, 0:96] if hop in T.cores else T.G2[:, 96 * t:96 * t + 96]
+        dv = X("VO")
+        issue("g", lambda: _send(g, T, topo, core, hop, out, dv[0], "rin%d" % t, "rl%d" % t), dv[1], [], sem="rl%d" % t, val=NE)
 
     V = X("CAT", 256, 384)
     S6 = X("FX", 207, 288, 16)
@@ -438,35 +442,45 @@ def rank_program(g, core, T, topo):
         hop = dst if topo.may_write(core, dst) else _relay(core, T, topo)
         if t:
             ts(X("TA"), X("ZN"), col("ACOL", 0), OP.add)
+            tc(IND(X("xt"), X("DLU", 6, 12)), X("N3", 896, 992))
             ts(X("TR", 0, 128), X("TA"), 4095, OP.bitwise_and)
             tc(X("LU", 0, 128), X("TR", 0, 128))
-            tt(X("FX", 972, 978), X("DN", 0, 6), X("FX", 980, 986), OP.mult)
-            tt(X("FX", 972, 978), X("FX", 972, 978), X("DMP6"), OP.add)
-            ts(X("DLU", 6, 12), X("FX", 972, 978), -1.0, OP.add)
-            tc(IND(X("xt"), X("DLU", 6, 12)), X("N3", 896, 992))
         gs(0, 0)
         gv(0, 0)
         gs(0, 1)
         if t:
-            newv()
-        vsplit()
+            ts(X("TA"), X("WI"), col("ACOL", 0), OP.add)
+            hurt(0)
+            ts(X("VCI"), X("TA"), 4095, OP.bitwise_and)
+            hurt(1)
+        ts(X("VM"), X("VCI"), KM, OP.add)
+        if t:
+            hurt(2)
+        tc(X("VHI"), X("VCI"))
         mm(X("PB3", 0, 256), X("KR2"), X("CLSR"), True, False)
         mm(X("PB3", 0, 256), X("KR3"), X("ONE"), False, False)
-        for h in range(2):
-            mm(X("PB3", h, 256, 2), X("HS%d" % h), X("VHI"), False, False)
-            mm(X("PB3", h, 256, 2), X("HS%d" % h), X("VLO"), False, False)
         smax(0)
         diff(0, "Z0")
         absz(0, "Z1")
         usum(0)
+        tt(X("VLO"), X("VCI"), X("VHI"), OP.subtract)
+        for h in range(2):
+            mm(X("PB3", h, 256, 2), X("HS%d" % h), X("VHI"), False, False)
+            mm(X("PB3", h, 256, 2), X("HS%d" % h), X("VLO"), False, False)
+        if t:
+            hurt(3)
         gv(0, 1)
         if t:
-            hurt()
+            hurt(4)
         smax(1)
         diff(1, "Z0")
         absz(1, "Z1")
         usum(1)
-        list1(0)
+        tt(X("T1", 0, 64), X("SQ", 0, 64), X("VM", 0, 64), OP.add)
+        if t:
+            hurt(5)
+        ts(X("TR", 128, 192), X("T1", 0, 64), 4095, OP.bitwise_and)
+        tc(X("LU", 128, 192), X("TR", 128, 192))
         gs(1, 0)
         gv(1, 0)
         list1(1)
@@ -475,29 +489,35 @@ def rank_program(g, core, T, topo):
         diff(0, "Z1")
         gv(1, 1)
         absz(0, "Z2")
-        ts(X("GE", 0, 128), X("Z2", 0, 128), col("THF", t), OP.is_ge)
+        act(X("GE", 0, 128), X("Z2", 0, 128), AF.Sign, bias=col("NTH", t))
         if t:
-            back(t - 1)
+            thaw1()
         smax(1)
         diff(1, "Z1")
         absz(1, "Z2")
-        ts(X("GE", 128, 256), X("Z2", 128, 256), col("THF", t), OP.is_ge)
-        if t:
-            thaw()
+        act(X("GE", 128, 256), X("Z2", 128, 256), AF.Sign, bias=col("NTH", t))
         mm(X("PB2", 0, 128), X("WU0"), X("GE", 0, 256, 2), True, False)
-        mm(X("PB2", 0, 128), X("WU1"), X("GE", 1, 256, 2), False, not t)
+        mm(X("PB2", 0, 128), X("WU1"), X("GE", 1, 256, 2), False, True)
         if t:
-            mm(X("PB2", 0, 128), X("N32"), X("FR"), False, True)
+            back(t - 1)
+            thaw2()
+            ts(X("FLX"), X("PB2", 0, 128), 1.0, OP.is_lt, 65536.0, OP.mult)
+            tt(X("FL"), X("PB7", 128, 256), X("FLX"), OP.is_gt)
+        else:
+            ts(X("FL"), X("PB2", 0, 128), 1.0, OP.is_ge)
         mm(X("PB3", 0, 128), X("ID"), X("Z2", 0, 128), False, False)
         mm(X("PB3", 128, 256), X("ID"), X("Z2", 128, 256), False, True)
         act(X("XF"), X("PB3", 0, 256), AF.Copy)
-        ts(X("FL"), X("PB2", 0, 128), 8.5, OP.is_ge)
         scan(X("INC"), X("FL"), X("ZER"), OP.add, OP.add)
         mm(X("PB2", 128, 256), X("KR1"), X("ONE", 0, 128), True, False)
         mm(X("PB2", 128, 256), X("RK2"), X("FL"), False, False)
         mm(X("PB2", 128, 256), X("M1K"), X("FL"), False, False)
         mm(X("PB2", 128, 256), X("RK1"), X("INC"), False, True)
+        if t:
+            ts(X("FR"), X("PB7", 128, 256), 0.0, OP.is_equal)
         tt(X("OFFP"), X("PB2", 128, 256), X("DUMPP"), OP.min)
+        if t:
+            ts(X("NF4"), X("PB7", 128, 256), 0.0, OP.is_gt, 4096.0, OP.mult)
         for e in range(8):
             mm(X("PB2", 256, 272), X("PL", 128 * e, 128 * e + 128), X("OFFP", e, 128, 8), e == 0, e == 7)
         tc(X("OL"), X("PB2", 256, 272))
@@ -507,30 +527,31 @@ def rank_program(g, core, T, topo):
               sv[1], [], sem="xl%d" % t, val=NE)
         if t == 0:
             consts_verdict()
-        ts(X("GO"), X("OFFP"), 95.5, OP.is_lt)
-        ts(X("P1"), X("TR"), 1.0, OP.add)
+        ts(X("GO"), X("OFFP"), 95.5, OP.is_ge, 4096.0, OP.mult)
         if t == 0:
             for b in range(2):
-                tt(X("LG", 128 * b, 128 * b + 128), X("P1", 128 * b, 128 * b + 128), X("GO"), OP.mult)
-            ts(X("NF2"), X("GO"), -1.0, OP.add)
+                tt(X("LG", 128 * b, 128 * b + 128), X("TR", 128 * b, 128 * b + 128), X("GO"), OP.add)
+            ts(X("NF2"), X("GO"), 1.0, OP.mult)
         else:
             for b in range(2):
-                tt(X("P1", 128 * b, 128 * b + 128), X("P1", 128 * b, 128 * b + 128), X("GO"), OP.mult)
-                tt(X("LG", 128 * b, 128 * b + 128), X("LG", 128 * b, 128 * b + 128), X("FR"), OP.mult)
-            tt(X("LG"), X("LG"), X("P1"), OP.add)
-            tt(X("NF2"), X("FR"), X("GO"), OP.add)
-            ts(X("NF2"), X("NF2"), -1.0, OP.add)
-        tc(X("LGU"), X("LG"))
-        if t:
-            tc(IND(X("D"), X("DLU", 0, 6)), X("ZER", 0, 96))
+                tt(X("LG", 128 * b, 128 * b + 128), X("LG", 128 * b, 128 * b + 128), X("NF4"), OP.add)
+                tt(X("P1", 128 * b, 128 * b + 128), X("TR", 128 * b, 128 * b + 128), X("GO"), OP.add)
             tt(X("SEL", 0, 128), V, X("VCI"), OP.subtract)
+            tt(X("LG"), X("LG"), X("P1"), OP.min)
             tt(X("SEL", 0, 128), X("SEL", 0, 128), X("FR"), OP.mult)
+            tt(X("NF2"), X("GO"), X("NF4"), OP.min)
+        ts(X("LGU"), X("LG"), 4096.0, OP.min)
+        if t:
             tt(V, X("SEL", 0, 128), X("VCI"), OP.add)
             tt(X("SEL", 128, 256), X("CAT", 128, 256), X("U1"), OP.subtract)
+            tc(IND(X("D"), X("DLU", 0, 6)), X("ZER", 0, 96))
             tt(X("SEL", 128, 256), X("SEL", 128, 256), X("FR"), OP.mult)
+            if t < STAGES - 1:
+                ms(X("XW", 0, 96), SENT)
             tt(X("CAT", 128, 256), X("SEL", 128, 256), X("U1"), OP.add)
         else:
             act(X("CAT", 128, 256), X("U1"), AF.Copy)
+            ms(X("XW", 0, 96), SENT)
         act(X("WT", 0, 128), V, AF.Square)
         act(X("WT", 128, 256), V, AF.Copy, scale=37.0)
         act(X("WT", 0, 128), X("WT", 0, 128), AF.Copy, bias=-0.25, scale=0.125)
@@ -538,24 +559,9 @@ def rank_program(g, core, T, topo):
         if t < STAGES - 1:
             tt(X("ZS"), X("WI"), X("S0I"), OP.add)
             ts(X("ZN"), X("ZS"), 4095, OP.bitwise_and)
-            ms(X("XW", 0, 96), SENT)
         if t == 0:
             consts_back()
             consts_out()
-        if t == STAGES - 1:
-            tc(X("CH"), X("CAT"))
-            tt(X("CL"), X("CAT"), X("CH"), OP.subtract)
-            for e in range(8):
-                mm(X("PB6", 256, 304), X("PL", 128 * e, 128 * e + 128), X("CH", e, 384, 8), e == 0, False)
-                mm(X("PB6", 256, 304), X("PL", 128 * e, 128 * e + 128), X("CL", e, 384, 8), False, e == 7)
-            tc(X("UL"), X("PB6", 256, 304))
-            tt(X("FX", 288, 544), IND(X("UL", 0, 32), X("YLU", 0, 16)), X("K8T"), OP.add)
-            act(X("FX", 544, 800), X("FX", 288, 544), AF.Square, scale=0.25)
-            tt(X("FX", 288, 544), X("FX", 544, 800), X("K2T"), OP.add)
-            tt(X("MS", 0, 256), IND(X("UL", 32, 48), X("YLU", 16, 32)), X("FX", 288, 544), OP.add)
-            ts(X("MS", 256, 512), X("MS", 0, 256), 4095, OP.bitwise_and)
-            tc(X("YO"), X("MS", 256, 512))
-            store("y", T.yt[:, :], X("YO"), "dyt")
         arrive("XR", 96 * t, 96 * t + 96, "xin%d" % t, NE)
         XR = X("XR", 96 * t, 96 * t + 96)
         Y1 = X("N3", 800, 896)
@@ -576,35 +582,52 @@ def rank_program(g, core, T, topo):
         mm(X("PB4", 0, 96), X("BOK"), X("E", 0, 96), False, True)
         tt(X("FX", 0, 96), X("PB4", 0, 96), Y1, OP.add)
         scan(X("FX", 192, 288), X("RST"), X("FX", 0, 96), OP.max, OP.min)
-        tc(X("DLU", 0, 6), S6)
+        ts(X("DLU", 0, 6), S6, -1.0, OP.add)
         tc(IND(X("D"), X("DLU", 0, 6)), X("CODE"))
-        A = 96
-        for b in range(2):
-            c0, q0 = 128 * b, 2048 * b
-            tc(X("G2", q0, q0 + 8 * A), IND(X("D"), X("LGU", c0, c0 + A // 2)))
-            cuts = [A, 256] if b == 0 else [A, 192, 256]
-            for p in range(len(cuts) - 1):
-                act(X("G2", q0 + 8 * cuts[p], q0 + 8 * cuts[p + 1]), IND(X("D"), X("LGU", c0 + cuts[p] // 2, c0 + cuts[p + 1] // 2)), AF.Copy)
-            for p0, p1 in zip([0] + cuts[:-1], cuts):
-                for l0 in range(64 * (p0 // 64), p1, 64):
-                    a0, a1, cl = max(l0, p0), min(l0 + 64, p1), l0 // 64
-                    for m in range(8):
-                        mm(X("PB%d" % (5 + b), 4 * (a0 - l0) + cl, 4 * (a1 - l0), 4), X("ID"), X("G2", q0 + 8 * a0 + m, q0 + 8 * a1, 8), m == 0, m == 7)
+
+        def piece(q, b, k0, k1):
+            o, i = X("G2", 2048 * b + 512 * k0, 2048 * b + 512 * k1), IND(X("D"), X("LGU", 128 * b + 32 * k0, 128 * b + 32 * k1))
+            if q == "v":
+                tc(o, i)
+            else:
+                act(o, i, AF.Copy)
+
+        def sums(b, k0, k1):
+            for cl in range(k0, k1):
+                for m in range(8):
+                    o = X("PB7", 0, 64) if b and cl == 3 else X("PB%d" % (5 + b), cl, 256, 4)
+                    mm(o, X("ID"), X("G2", 2048 * b + 512 * cl + m, 2048 * b + 512 * cl + 512, 8), m == 0, m == 7)
+
+        mm(X("PB6", 3, 256, 4), X("ID"), X("ZER", 0, 64), True, True)
+        piece("v", 0, 0, 2)
+        piece("s", 0, 2, 4)
+        piece("v", 1, 0, 1)
+        piece("s", 1, 1, 3)
+        piece("s", 1, 3, 4)
+        sums(0, 0, 2)
+        sums(0, 2, 4)
+        sums(1, 0, 1)
+        sums(1, 1, 3)
+        sums(1, 3, 4)
         ts(X("MS", 0, 96), XR, 21, OP.logical_shift_right)
         tt(X("FX", 0, 96), X("MS", 0, 96), X("DIAG"), OP.mult)
         scan(X("FX", 96, 192), X("HOLD"), X("FX", 0, 96), OP.mult, OP.add)
         for cl in range(1, 4):
             for p in (0, 4):
-                ts(X("FX", 900 + p + cl, 948, 8), X("FX", 111, 192, 16), float(cl), OP.is_ge, waw=False)
+                ts(X("FX", 900 + p + cl, 948, 8), X("FX", 111, 192, 16), float(cl), OP.is_ge, 8192.0, OP.mult, waw=False)
         ts(X("FX", 990, 996), S6, 4100.0, OP.is_ge, -1.0, OP.mult)
-        tt(X("FX", 980, 986), S6, X("DMP6"), OP.subtract)
         ts(X("N3", 896, 992), XR, 255, OP.bitwise_and)
         for b in range(2):
             ts(X("MS", 256 * b, 256 * b + 256), X("PB%d" % (5 + b), 0, 256), float(0x777777), OP.add)
             ts(X("N3", 256 * b, 256 * b + 256), X("MS", 256 * b, 256 * b + 256), 0x888888, OP.bitwise_and, 3, OP.logical_shift_right)
         tt(X("N3", 512, 768), X("N3", 0, 256), X("N3", 256, 512), OP.add)
+        ts(X("P1", 0, 64), X("PB7", 0, 64), float(0x777777), OP.add)
         tt(X("MS", 0, 128), X("N3", 512, 640), X("N3", 640, 768), OP.add)
+        ts(X("P1", 64, 128), X("P1", 0, 64), 0x888888, OP.bitwise_and, 3, OP.logical_shift_right)
         tt(X("MS", 128, 192), X("MS", 0, 64), X("MS", 64, 128), OP.add)
+        tt(X("P1", 128, 160), X("P1", 64, 96), X("P1", 96, 128), OP.add)
+        tt(X("P1", 160, 176), X("P1", 128, 144), X("P1", 144, 160), OP.add)
+        tt(X("MS", 131, 192, 4), X("MS", 131, 192, 4), X("P1", 160, 176), OP.add)
         ts(X("MS", 192, 256), X("MS", 128, 192), float(0x777777), OP.add)
         ts(X("MS", 256, 320), X("MS", 192, 256), 0x888888, OP.bitwise_and, 3, OP.logical_shift_right)
         tt(X("MS", 320, 352), X("MS", 256, 288), X("MS", 288, 320), OP.add)
@@ -613,15 +636,19 @@ def rank_program(g, core, T, topo):
         for k in range(6):
             ts(X("MS", 384 + 8 * k, 392 + 8 * k), X("MS", 368, 376), 4 * k, OP.logical_shift_right, 15, OP.bitwise_and)
         tt(X("FX", 1000, 1048), X("MS", 384, 432), X("FX", 900, 948), OP.mult)
-        tt(X("FX", 1048, 1072), X("FX", 1000, 1048, 2), X("FX", 1001, 1048, 2), OP.add)
-        tt(X("FX", 1072, 1084), X("FX", 1048, 1072, 2), X("FX", 1049, 1072, 2), OP.add)
-        tt(X("FX", 1060, 1066), X("FX", 1072, 1084, 2), X("FX", 1073, 1084, 2), OP.add)
-        tt(X("DN", 0, 6), X("FX", 1060, 1066), X("FX", 990, 996), OP.is_equal)
-        dv = X("DN", 0, 8)
-        issue("g", lambda: _send(g, T, topo, core, hop, T.RR[:, 8 * t:8 * t + 8], dv[0], "rin%d" % t, "rl%d" % t),
-              dv[1], [], sem="rl%d" % t, val=NE)
+        scan(X("FX", 1048, 1096), X("SEG", 0, 48), X("FX", 1000, 1048), OP.mult, OP.add)
+        vet = X("FX", 1055, 1096, 8)
+        tt(X("DN", 0, 6), vet, X("FX", 990, 996), OP.is_equal)
+        if t < STAGES - 1:
+            tt(X("FX", 972, 978), vet, S6, OP.add)
         mm(X("PB4", 128, 134), X("ONE", 0, 128), X("DN", 0, 6), True, True)
+        if t < STAGES - 1:
+            tt(X("FX", 980, 986), X("FX", 972, 978), X("DMP6"), OP.min)
         red(col("ACOL", 0), X("PB4", 128, 134))
+        if t < STAGES - 1:
+            ts(X("DLU", 6, 12), X("FX", 980, 986), -1.0, OP.add)
+        verdict_row(t, hop)
+        tt(X("N3", 515, 768, 4), X("N3", 515, 768, 4), X("P1", 64, 128), OP.add)
 
     newv()
     tc(X("VHI"), X("VCI"))
@@ -629,11 +656,27 @@ def rank_program(g, core, T, topo):
     for e in range(8):
         mm(X("PB3", 0, 16), X("PL", 128 * e, 128 * e + 128), X("VHI", e, 128, 8), e == 0, False)
         mm(X("PB3", 0, 16), X("PL", 128 * e, 128 * e + 128), X("VLO", e, 128, 8), False, e == 7)
-    hurt()
+    for k in range(6):
+        hurt(k)
+    thaw1()
     tc(X("FIN", 0, 16), X("PB3", 0, 16))
+    tc(X("CH"), X("CAT"))
+    tt(X("CL"), X("CAT"), X("CH"), OP.subtract)
+    for e in range(8):
+        mm(X("PB6", 256, 304), X("PL", 128 * e, 128 * e + 128), X("CH", e, 384, 8), e == 0, False)
+        mm(X("PB6", 256, 304), X("PL", 128 * e, 128 * e + 128), X("CL", e, 384, 8), False, e == 7)
+    tc(X("UL"), X("PB6", 256, 304))
+    tt(X("FX", 288, 544), IND(X("UL", 0, 32), X("YLU", 0, 16)), X("K8T"), OP.add)
+    act(X("FX", 544, 800), X("FX", 288, 544), AF.Square, scale=0.25)
     tt(X("FIN", 16, 32), X("UL", 32, 48), X("FIN", 0, 16), OP.subtract)
+    tt(X("FX", 288, 544), X("FX", 544, 800), X("K2T"), OP.add)
+    tt(X("MS", 0, 256), IND(X("UL", 32, 48), X("YLU", 16, 32)), X("FX", 288, 544), OP.add)
+    ts(X("MS", 256, 512), X("MS", 0, 256), 4095, OP.bitwise_and)
+    tc(X("YO"), X("MS", 256, 512))
+    store("y", T.yt[:, :], X("YO"), "dyt")
     back(STAGES - 1)
-    thaw()
+    thaw2()
+    ts(X("FR"), X("PB7", 128, 256), 0.0, OP.is_equal)
     for e in range(8):
         mm(X("PB2", 0, 16), X("PL", 128 * e, 128 * e + 128), X("FR", e, 128, 8), e == 0, e == 7)
     tc(X("YS", 16, 32), X("PB2", 0, 16))

from concourse.bass import DstId
from concourse.mybir import AluOpType as OP, AxisListType, ActivationFunctionType as AF

KAP = (3, 29, 71, 113, 151, 197, 233, 277)
STAGES, CAP = 4, 96
NE = 8
DUMP = 4112
NV, NSC = 40, 88
SENT = 8191 * 256

_F, _B, _I, _U = "float32", "bfloat16", "int32", "uint16"


def _sb(n, d):
    return ("sbuf", [128, n], d)


SCRATCH = {
    "xt": _sb(4224, _B), "D": _sb(4224, _B), "Z0": _sb(256, _B), "Z1": _sb(256, _B), "Z2": _sb(256, _B),
    "V0": _sb(16, _I), "THI": _sb(4, _I), "NTH": _sb(4, _F),
    "GT": _sb(2048, _B), "HM": _sb(2048, _B), "SEG": _sb(1024, _B), "G2": _sb(4096, _B),
    "CJ": _sb(128, _F), "GJ": _sb(128, _F), "GH": _sb(128, _F), "GM": _sb(128, _F), "TJ": _sb(128, _F),
    "IS": _sb(96, _F), "K96": _sb(96, _F), "PI": _sb(1, _I), "PT": _sb(5, _I), "PC": _sb(5, _F), "DC": _sb(8, _F),
    "BE": _sb(8, _F), "PQ": _sb(8, _F), "KROW": _sb(8, _F), "KEQ": _sb(8, _F), "KC": _sb(4, _F), "RI": _sb(16, _F),
    "CLSR": _sb(256, _B), "DUMPP": _sb(128, _F), "DPT": _sb(128, _F),
    "BO": _sb(128, _B), "BOK": _sb(128, _B), "WU0": _sb(128, _B), "WU1": _sb(128, _B), "ID": _sb(128, _B), "NI": _sb(128, _B),
    "NF4": _sb(128, _B), "M1K": _sb(128, _B), "RK1": _sb(128, _B), "RK2": _sb(128, _B), "RT1": _sb(128, _B), "RT2": _sb(128, _B),
    "PL": _sb(1024, _B), "LP": _sb(1024, _B), "HS0": _sb(128, _B), "HS1": _sb(128, _B), "RS": _sb(2048, _B),
    "VS0": _sb(128, _B), "VS1": _sb(128, _B), "FLX": _sb(128, _B), "KR1": _sb(128, _B), "KR2": _sb(128, _B), "KR3": _sb(128, _B),
    "ONE": _sb(256, _B), "ZER": _sb(128, _B), "DIAG": _sb(96, _F), "HOLD": _sb(96, _F), "RST": _sb(96, _F), "OB": _sb(96, _B),
    "R0M": _sb(96, _F), "CODE": _sb(96, _B), "DMP6": _sb(6, _F), "W6": _sb(6, _F), "K8T": _sb(256, _F), "K2T": _sb(256, _F),
    "YLI": _sb(32, _I), "YLU": _sb(32, _U),
    "VH0": _sb(16, _B), "VL0": _sb(16, _B), "S0F": _sb(128, _F), "S0I": _sb(128, _I),
    "CAT": _sb(384, _F), "CH": _sb(384, _B), "CL": _sb(384, _B), "U1": _sb(128, _F), "SQ": _sb(128, _F),
    "TA": _sb(128, _I), "T1": _sb(128, _I), "TR": _sb(256, _I), "LU": _sb(256, _U), "VCI": _sb(128, _I), "VM": _sb(128, _F),
    "VHI": _sb(128, _B), "VLO": _sb(128, _B), "GE": _sb(256, _B), "FL": _sb(128, _B), "INC": _sb(128, _B), "OFFP": _sb(128, _B),
    "OL": _sb(16, _U), "XF": _sb(256, _F), "XW": _sb(1024, _I), "GO": _sb(128, _B), "FR": _sb(128, _B), "NF2": _sb(128, _B),
    "P1": _sb(256, _I), "LG": _sb(256, _I), "LGU": _sb(256, _U), "WT": _sb(384, _F), "WI": _sb(128, _I), "ZS": _sb(128, _I),
    "ZN": _sb(128, _I), "SEL": _sb(256, _F),
    "XR": _sb(384, _I), "VO": _sb(96, _B), "MS": _sb(512, _I), "VWIN": _sb(1024, _B),
    "E": _sb(336, _B), "FX": _sb(1152, _F), "N3": _sb(1024, _I), "DLU": _sb(12, _U), "DN": _sb(8, _B), "HB": _sb(256, _B),
    "VROW": _sb(256, _B), "ACOL": _sb(4, _F), "UL": _sb(48, _F), "YO": _sb(256, _F), "YS": _sb(32, _F), "FIN": _sb(96, _F),
}
for _k in range(8):
    SCRATCH["PB%d" % _k] = ("psum", [128, 512], "float32")

SEMAPHORES = ["qv", "qs", "qp", "qg", "dx", "dsd", "dv0", "dth", "dyt", "dys"] + [n + str(t) for t in range(STAGES) for n in ("xin", "rin", "xl", "rl")]


def _partner(r, t):
    return r ^ (1 + t % 3)


def _relay(c, T, topo):
    r = T.rank_of(c)
    far = [T.cores[_partner(r, t)] for t in range(STAGES)]
    far = [d for d in far if not topo.may_write(c, d)]
    if not far:
        return None
    ks = [k for k in topo.cores_of(c) if k not in T.cores and topo.may_write(c, k) and all(topo.may_write(k, d) for d in far)]
    ks.sort(key=lambda k: (topo.die(k) != topo.die(c), k))
    return ks[0]


def _send(g, T, topo, src, dst, out, in_, rsem, lsem):
    eng = [e for e in topo.engines(src, dst)][:NE]
    m = 0
    for e in eng:
        m |= 1 << e
    rid, pid = topo.addr(dst, src)
    g.remote_dma(out, in_, remote_sem=T.sem[rsem], local_sem=T.sem[lsem], pid=pid, routing_id=rid, dma_engine_mask=m)


def _relay_program(g, core, T, topo, c):
    r = T.rank_of(c)
    used = []
    for t in range(STAGES):
        d = T.cores[_partner(r, t)]
        if topo.may_write(c, d):
            continue
        g.wait_ge(T.sem["xin%d" % t], NE)
        _send(g, T, topo, core, d, T.XR[:, 96 * t:96 * t + 96], T.XR[:, 96 * t:96 * t + 96], "xin%d" % t, "xl%d" % t)
        g.wait_ge(T.sem["rin%d" % t], NE)
        _send(g, T, topo, core, d, T.VWIN[:, 0:96], T.G2[:, 96 * t:96 * t + 96], "rin%d" % t, "rl%d" % t)
        used.append(t)
    for t in used:
        g.wait_ge(T.sem["xl%d" % t], NE)
        g.wait_ge(T.sem["rl%d" % t], NE)


def rank_program(g, core, T, topo):
    rank = T.rank_of(core)
    if rank is None:
        for c in T.cores:
            if core in topo.cores_of(c) and _relay(c, T, topo) == core:
                _relay_program(g, core, T, topo, c)
        return

    Q = {"v": g.vector, "s": g.scalar, "p": g.tensor, "g": g, "y": g.sync}
    CNT = {"v": 0, "s": 0, "p": 0, "g": 0}
    clk = {q: {} for q in Q}
    acc = {}
    idx = [0]

    def X(name, a=0, b=None, st=1):
        n = SCRATCH[name][1][1]
        b = n if b is None else b
        return (T[name][:, a:b:st] if st != 1 else T[name][:, a:b], [(name, a, b)])

    def IND(win, off):
        return (win[0].indirect(off[0]), win[1], off[1])

    def wait(q, rec):
        if clk[q].get(rec["sem"], 0) >= rec["val"]:
            return
        Q[q].wait_ge(T.sem[rec["sem"]], rec["val"])
        for k, n in rec["snap"].items():
            if clk[q].get(k, 0) < n:
                clk[q][k] = n
        clk[q][rec["sem"]] = rec["val"]

    def issue(q, fn, reads, writes, sem=None, val=None, waw=True):
        lab = q if sem is None else "dma"
        deps = []
        for kind, regs in (("r", reads), ("w", writes)):
            for (nm, lo, hi) in regs:
                ps = nm[:2] == "PB"
                for rec in acc.get(nm, []):
                    if not ps and (rec["hi"] <= lo or rec["lo"] >= hi):
                        continue
                    if rec["q"] == lab and lab != "dma":
                        if q == "p" and ps:
                            continue
                        if kind == "r" and not rec["w"]:
                            continue
                        if kind == "w" and not waw:
                            continue
                        if ps and (rec["hi"] <= lo or rec["lo"] >= hi):
                            continue
                        deps.append(rec)
                    elif rec["w"] or kind == "w" or ps:
                        deps.append(rec)
        deps.sort(key=lambda r: -r["idx"])
        for rec in deps:
            wait(q, rec)
        ins = fn()
        if sem is None:
            CNT[q] += 1
            ins.then_inc(T.sem["q" + q], 1)
            s, n = "q" + q, CNT[q]
        else:
            s, n = sem, val
            if ins is not None and val == 16:
                ins.then_inc(T.sem[sem], 16)
        snap = dict(clk[q])
        idx[0] += 1
        for w, regs in ((False, reads), (True, writes)):
            for (nm, lo, hi) in regs:
                old = acc.get(nm, [])
                if w:
                    old = [r for r in old if not (lo <= r["lo"] and r["hi"] <= hi)]
                else:
                    old = [r for r in old if r["w"] or not (r["q"] == lab and lab != "dma" and lo <= r["lo"] and r["hi"] <= hi)]
                old.append({"lo": lo, "hi": hi, "w": w, "q": lab, "sem": s, "val": n, "snap": snap, "idx": idx[0]})
                acc[nm] = old

    def arrive(name, a, b, sem, val):
        idx[0] += 1
        acc.setdefault(name, []).append({"lo": a, "hi": b, "w": True, "q": "dma", "sem": sem, "val": val, "snap": {}, "idx": idx[0]})

    def rd(*vs):
        out = []
        for v in vs:
            if isinstance(v, tuple):
                out += v[1]
                if len(v) == 3:
                    out += v[2]
        return out

    def ap(v):
        return v[0] if isinstance(v, tuple) else v

    def outs(o):
        return o[1], (o[2] if len(o) == 3 else [])

    def tt(o, a, b, op, waw=True):
        w, r = outs(o)
        issue("v", lambda: g.vector.tensor_tensor(ap(o), ap(a), ap(b), op), rd(a, b) + r, w, waw=waw)

    def ts(o, a, s1, op0, s2=None, op1=None, waw=True):
        def f():
            if op1 is None:
                return g.vector.tensor_scalar(ap(o), ap(a), ap(s1), None, op0)
            return g.vector.tensor_scalar(ap(o), ap(a), ap(s1), ap(s2), op0, op1)
        issue("v", f, rd(a, s1, s2), o[1], waw=waw)

    def tc(o, a):
        w, r = outs(o)
        issue("v", lambda: g.vector.tensor_copy(ap(o), ap(a)), rd(a) + r, w)

    def ms(o, c):
        issue("v", lambda: g.vector.memset(ap(o), c), [], o[1], waw=True)

    def scan(o, d0, d1, op0, op1):
        issue("v", lambda: g.vector.tensor_tensor_scan(ap(o), ap(d0), ap(d1), 0.0, op0, op1), rd(d0, d1), o[1])

    def red(o, a):
        issue("v", lambda: g.vector.tensor_reduce(ap(o), ap(a), AxisListType.X, OP.add), rd(a), o[1])

    def act(o, a, func, bias=0.0, scale=1.0):
        issue("s", lambda: g.scalar.activation(ap(o), ap(a), func, bias=ap(bias), scale=ap(scale)), rd(a, bias, scale), o[1])

    def mm(o, l, r, start, stop):
        issue("p", lambda: g.tensor.matmul(ap(o), ap(l), ap(r), start, stop), rd(l, r), o[1])

    def iota(o, pat, base=0, cm=0):
        def f():
            if SCRATCH[o[1][0][0]][2] == "int32":
                return g.iota(ap(o), pat, base, cm)
            return g.iota(ap(o), pat, base, cm, allow_small_or_imprecise_dtypes=True)
        issue("g", f, [], o[1])

    def load(q, name, a, b, src, sem):
        v = X(name, a, b)
        issue(q, lambda: Q[q].dma_start(v[0], src), [], v[1], sem=sem, val=16)

    def store(q, dst, v, sem):
        issue(q, lambda: Q[q].dma_start(dst, v[0]), v[1], [], sem=sem, val=16)

    def col(name, j):
        return X(name, j, j + 1)

    load("s", "Z0", 0, 256, T.sd[:, :], "dsd")
    load("y", "V0", 0, 16, T.v0[:, :], "dv0")
    load("y", "xt", 0, 4096, T.x[:, :], "dx")
    load("s", "THI", 0, 4, T.th[:, :], "dth")

    iota(X("PI"), [[0, 1]], 0, 1)
    iota(X("GH"), [[8, 16], [0, 8]])
    iota(X("IS"), [[0, 6], [1, 16]])
    iota(X("TJ"), [[16, 8], [1, 2], [0, 8]])
    iota(X("PQ"), [[-2, 8]], 0, 1)
    iota(X("CJ"), [[1, 128]])
    iota(X("GJ"), [[16, 8], [0, 16]])
    iota(X("GM"), [[16, 8], [0, 2], [1, 8]])
    iota(X("BE"), [[2, 8]])
    iota(X("DPT", 0, 64), [[4, 64]], 256)
    iota(X("DPT", 64, 128), [[8, 64]], 512)
    iota(X("CLSR"), [[1, 4], [0, 64]])
    iota(X("K96"), [[16, 6], [0, 16]], DUMP)
    iota(X("HM", 0, 1024), [[0, 128], [1, 8]])
    iota(X("VWIN", 96, 1024), [[0, 928]])
    iota(X("D"), [[0, 4224]])

    for m in range(8):
        ms(col("KROW", m), float(KAP[m]))
    ms(X("xt", 4096, 4224), 0.0)
    P, I16, M8, H2, G16 = [col("PC", j) for j in range(5)]
    tc(col("PT", 0), X("PI"))
    ts(col("PT", 1), X("PI"), 15, OP.bitwise_and)
    ts(col("PT", 2), X("PI"), 7, OP.bitwise_and)
    ts(col("PT", 3), X("PI"), 3, OP.logical_shift_right, 1, OP.bitwise_and)
    ts(col("PT", 4), X("PI"), 112, OP.bitwise_and)
    tc(X("PC"), X("PT"))
    ts(col("DC", 0), G16, 8.0, OP.add)
    ts(X("WU0"), X("GH"), G16, OP.is_equal)
    ts(X("WU1"), X("GH"), col("DC", 0), OP.is_equal)
    ts(X("KEQ"), X("IS", 0, 8), M8, OP.is_equal)
    tt(X("KEQ"), X("KEQ"), X("KROW"), OP.mult)
    red(col("KC", 0), X("KEQ"))
    ts(col("KC", 1), col("KC", 0), 2.0, OP.mult)
    tt(col("KC", 2), col("KC", 1), col("KC", 1), OP.mult)
    ts(col("KC", 2), col("KC", 2), -1.0, OP.mult, -0.25, OP.add)
    K2, KM = col("KC", 1), col("KC", 2)
    for e in range(8):
        ts(X("LP", 128 * e, 128 * e + 128), X("TJ"), col("PQ", e), OP.is_equal)
    tc(X("VH0"), X("V0"))
    tt(X("VL0"), X("V0"), X("VH0"), OP.subtract)

    mm(X("PB0", 0, 128), X("WU0"), X("Z0", 0, 256, 2), True, False)
    mm(X("PB0", 0, 128), X("WU1"), X("Z0", 1, 256, 2), False, True)
    act(X("S0F"), X("PB0", 0, 128), AF.Square, bias=K2, scale=0.25)
    act(X("CAT", 0, 128), X("PB0", 0, 128), AF.Copy)
    act(X("SEG"), X("HM", 0, 1024), AF.Sign)
    for e in range(8):
        mm(X("PB1", e, 128, 8), X("LP", 128 * e, 128 * e + 128), X("VH0"), True, False)
        mm(X("PB1", e, 128, 8), X("LP", 128 * e, 128 * e + 128), X("VL0"), False, True)
    ts(X("S0I"), X("S0F"), KM, OP.add)
    tc(X("VCI"), X("PB1", 0, 128))
    tt(X("TA"), X("S0I"), X("VCI"), OP.add)
    ts(X("TR", 0, 128), X("TA"), 4095, OP.bitwise_and)
    tc(X("LU", 0, 128), X("TR", 0, 128))
    ts(X("ID"), X("CJ"), P, OP.is_equal)
    ts(X("NI"), X("CJ"), P, OP.is_equal, -1.0, OP.mult)
    tc(X("CAT", 256, 384), X("VCI"))
    ts(X("NTH"), X("THI"), -1.0, OP.mult, 0.5, OP.add)

    ts(X("BO"), X("GJ"), G16, OP.is_equal)
    tt(col("DC", 1), G16, M8, OP.add)
    ts(col("DC", 2), M8, 0.0, OP.is_equal)
    tt(col("DC", 3), G16, H2, OP.add)
    ts(col("DC", 4), H2, -1.0, OP.mult, 1.0, OP.add)
    ts(col("DC", 5), H2, -1.0, OP.mult)
    ts(col("DC", 6), col("DC", 2), col("DC", 4), OP.mult, 256.0, OP.mult)
    ts(col("DC", 7), col("DC", 2), H2, OP.mult, 256.0, OP.mult)
    ts(X("RK1"), X("GM"), col("DC", 1), OP.is_equal)
    act(X("RT1"), X("RK1"), AF.Identity, scale=col("DC", 5))
    act(X("RT2"), X("NI"), AF.Identity, scale=col("DC", 4))
    act(X("M1K"), X("NI"), AF.Copy, scale=1024.0)
    act(X("HS0"), X("BO"), AF.Identity, scale=col("DC", 6))
    act(X("HS1"), X("BO"), AF.Identity, scale=col("DC", 7))
    ts(X("RI"), X("IS", 0, 16), I16, OP.is_equal)
    ms(X("KR1"), 8.0)
    ms(X("KR2"), 16384.0)
    ms(X("KR3"), 2.0)
    ms(X("ONE"), 1.0)
    ms(X("ZER"), 0.0)
    ts(X("BE"), X("BE"), col("DC", 3), OP.add)
    for e in range(8):
        ts(X("PL", 128 * e, 128 * e + 128), X("CJ"), col("BE", e), OP.is_equal, col("DC", 2), OP.mult)
    ts(col("ACOL", 1), H2, 2.0, OP.mult)
    ts(col("ACOL", 2), H2, 4.0, OP.mult)
    ts(X("DUMPP", 0, 64), X("DPT", 0, 64), col("ACOL", 1), OP.add)
    ts(X("DUMPP", 64, 128), X("DPT", 64, 128), col("ACOL", 2), OP.add)
    ms(X("XW", 0, 96), SENT)
    tt(X("RK2"), X("RT1"), X("RT2"), OP.add)

    def consts_verdict():
        ts(X("DIAG"), X("IS"), I16, OP.is_equal)
        ts(X("HOLD"), X("IS"), 0.0, OP.is_gt)
        act(X("OB"), X("DIAG"), AF.Copy, bias=57344.0, scale=-65536.0)
        act(X("BOK"), X("BO"), AF.Copy, scale=8192.0)
        ts(X("R0M"), X("IS"), 0.0, OP.is_equal)
        ts(X("RST"), X("K96"), I16, OP.add)
        tc(X("DMP6"), X("RST", 0, 96, 16))
        tt(X("RST"), X("RST"), X("R0M"), OP.mult)
        for k in range(6):
            act(X("CODE", 16 * k, 16 * k + 16), X("DIAG", 16 * k, 16 * k + 16), AF.Copy, scale=float(16 ** k))
            ms(col("W6", k), float(2 * 16 ** k))
        ms(X("FX", 900, 948, 4), 8192.0)

    def consts_back():
        for i in range(16):
            act(X("RS", 128 * i, 128 * i + 128), X("BO"), AF.Identity, scale=col("RI", i))
        act(X("VS0"), X("WU0"), AF.Identity, scale=col("RI", 0))
        act(X("VS1"), X("WU1"), AF.Identity, scale=col("RI", 0))

    def consts_out():
        for e in range(16):
            act(X("K8T", 16 * e, 16 * e + 16), X("IS", 0, 16), AF.Copy, bias=float(8 * KAP[e % 8]), scale=0.0)
        act(X("K2T"), X("K8T"), AF.Square, scale=0.25)
        act(X("K2T"), X("K2T"), AF.Copy, bias=-0.25, scale=-1.0)
        ms(X("YLI"), 0)
        ts(X("YLI", 0, 8), X("YLI", 0, 8), I16, OP.add)
        ts(X("YLI", 8, 16), X("YLI", 8, 16), I16, OP.add, 16.0, OP.add)
        ts(X("YLI", 16, 32), X("YLI", 16, 32), I16, OP.add)
        tc(X("YLU"), X("YLI"))

    def gs(b, bt):
        l0 = 128 * bt
        c0 = 128 * b + l0 // 2
        act(X("GT", 8 * l0, 8 * (l0 + NSC)), IND(X("xt"), X("LU", c0, c0 + NSC // 2)), AF.Copy)

    def gv(b, bt):
        l0 = 128 * bt + NSC
        c0 = 128 * b + l0 // 2
        tc(X("GT", 8 * l0, 8 * (l0 + NV)), IND(X("xt"), X("LU", c0, c0 + NV // 2)))

    def smax(bt):
        a = 1024 * bt
        scan(X("HM", a, a + 1024), X("SEG"), X("GT", a, a + 1024), OP.mult, OP.max)

    def diff(bt, zin):
        l0 = 128 * bt
        pb = "PB%d" % bt
        mm(X(pb, 0, 128), X("NI"), X(zin, l0, l0 + 128), True, False)
        mm(X(pb, 0, 128), X("ID"), X("HM", 8 * l0 + 7, 8 * l0 + 1024, 8), False, True)

    def absz(bt, zout):
        l0 = 128 * bt
        act(X(zout, l0, l0 + 128), X("PB%d" % bt, 0, 128), AF.Abs)

    def usum(bt):
        l0, c0 = 128 * bt, 64 * bt
        pb = "PB%d" % bt
        mm(X(pb, 128, 192), X("WU0"), X("Z1", l0, l0 + 128, 2), True, False)
        mm(X(pb, 128, 192), X("WU1"), X("Z1", l0 + 1, l0 + 128, 2), False, True)
        act(X("SQ", c0, c0 + 64), X(pb, 128, 192), AF.Square, bias=K2, scale=0.25)
        act(X("U1", c0, c0 + 64), X(pb, 128, 192), AF.Copy)

    def list1(bt):
        c0 = 64 * bt
        tt(X("T1", c0, c0 + 64), X("SQ", c0, c0 + 64), X("VM", c0, c0 + 64), OP.add)
        ts(X("TR", 128 + c0, 192 + c0), X("T1", c0, c0 + 64), 4095, OP.bitwise_and)
        tc(X("LU", 128 + c0, 192 + c0), X("TR", 128 + c0, 192 + c0))

    def newv():
        ts(X("TA"), X("WI"), col("ACOL", 0), OP.add)
        ts(X("VCI"), X("TA"), 4095, OP.bitwise_and)

    def hurt(step):
        if step == 0:
            tt(X("FX", 960, 966), X("DN", 0, 6), X("W6"), OP.mult)
        elif step == 1:
            red(col("FX", 966), X("FX", 960, 966))
        elif step == 2:
            ts(col("FX", 967), col("FX", 966), float(0x111111), OP.add)
        elif step == 3:
            ts(X("MS", 0, 256), X("N3", 512, 768), col("FX", 967), OP.add)
        elif step == 4:
            ts(X("MS", 256, 512), X("MS", 0, 256), 0x444444, OP.bitwise_and)
        else:
            ts(X("HB"), X("MS", 256, 512), 0.0, OP.is_gt)

    def back(t):
        arrive("VWIN", 0, 96, "rin%d" % t, NE)
        act(X("VROW"), IND(X("VWIN"), X("OL")), AF.Copy)

    def thaw1():
        mm(X("PB7", 128, 256), X("ID"), X("NF2"), True, False)
        for cl in range(4):
            for h in range(2):
                mm(X("PB7", 128 + 32 * cl, 160 + 32 * cl), X("WU%d" % h), X("HB", 4 * h + cl, 256, 8), False, False)

    def thaw2():
        mm(X("PB7", 128, 256), X("VS0"), X("VROW", 0, 256, 2), False, False)
        mm(X("PB7", 128, 256), X("VS1"), X("VROW", 1, 256, 2), False, True)

    def verdict_row(t, hop):
        for i in range(16):
            mm(X("PB7", i, 96, 16), X("RS", 128 * i, 128 * i + 128), X("DN", 0, 6), True, True)
        act(X("VO"), X("PB7", 0, 96), AF.Copy, bias=1.0, scale=-1.0)
        out = T.VWIN[:, 0:96] if hop in T.cores else T.G2[:, 96 * t:96 * t + 96]
        dv = X("VO")
        issue("g", lambda: _send(g, T, topo, core, hop, out, dv[0], "rin%d" % t, "rl%d" % t), dv[1], [], sem="rl%d" % t, val=NE)

    V = X("CAT", 256, 384)
    S6 = X("FX", 207, 288, 16)

    for t in range(STAGES):
        dst = T.cores[_partner(rank, t)]
        hop = dst if topo.may_write(core, dst) else _relay(core, T, topo)
        if t:
            ts(X("TA"), X("ZN"), col("ACOL", 0), OP.add)
            tc(IND(X("xt"), X("DLU", 6, 12)), X("N3", 896, 992))
            ts(X("TR", 0, 128), X("TA"), 4095, OP.bitwise_and)
            tc(X("LU", 0, 128), X("TR", 0, 128))
        gs(0, 0)
        gv(0, 0)
        gs(0, 1)
        if t:
            ts(X("TA"), X("WI"), col("ACOL", 0), OP.add)
            hurt(0)
            ts(X("VCI"), X("TA"), 4095, OP.bitwise_and)
            hurt(1)
        ts(X("VM"), X("VCI"), KM, OP.add)
        if t:
            hurt(2)
        tc(X("VHI"), X("VCI"))
        mm(X("PB3", 0, 256), X("KR2"), X("CLSR"), True, False)
        mm(X("PB3", 0, 256), X("KR3"), X("ONE"), False, False)
        smax(0)
        diff(0, "Z0")
        absz(0, "Z1")
        usum(0)
        tt(X("VLO"), X("VCI"), X("VHI"), OP.subtract)
        for h in range(2):
            mm(X("PB3", h, 256, 2), X("HS%d" % h), X("VHI"), False, False)
            mm(X("PB3", h, 256, 2), X("HS%d" % h), X("VLO"), False, False)
        if t:
            hurt(3)
        gv(0, 1)
        if t:
            hurt(4)
        smax(1)
        diff(1, "Z0")
        absz(1, "Z1")
        usum(1)
        tt(X("T1", 0, 64), X("SQ", 0, 64), X("VM", 0, 64), OP.add)
        if t:
            hurt(5)
        ts(X("TR", 128, 192), X("T1", 0, 64), 4095, OP.bitwise_and)
        tc(X("LU", 128, 192), X("TR", 128, 192))
        gs(1, 0)
        gv(1, 0)
        list1(1)
        gs(1, 1)
        smax(0)
        diff(0, "Z1")
        gv(1, 1)
        absz(0, "Z2")
        act(X("GE", 0, 128), X("Z2", 0, 128), AF.Sign, bias=col("NTH", t))
        if t:
            thaw1()
        smax(1)
        diff(1, "Z1")
        absz(1, "Z2")
        act(X("GE", 128, 256), X("Z2", 128, 256), AF.Sign, bias=col("NTH", t))
        mm(X("PB2", 0, 128), X("WU0"), X("GE", 0, 256, 2), True, False)
        mm(X("PB2", 0, 128), X("WU1"), X("GE", 1, 256, 2), False, True)
        if t:
            back(t - 1)
            thaw2()
            ts(X("FLX"), X("PB2", 0, 128), 1.0, OP.is_lt, 65536.0, OP.mult)
            tt(X("FL"), X("PB7", 128, 256), X("FLX"), OP.is_gt)
        else:
            ts(X("FL"), X("PB2", 0, 128), 1.0, OP.is_ge)
        mm(X("PB3", 0, 128), X("ID"), X("Z2", 0, 128), False, False)
        mm(X("PB3", 128, 256), X("ID"), X("Z2", 128, 256), False, True)
        act(X("XF"), X("PB3", 0, 256), AF.Copy)
        scan(X("INC"), X("FL"), X("ZER"), OP.add, OP.add)
        mm(X("PB2", 128, 256), X("KR1"), X("ONE", 0, 128), True, False)
        mm(X("PB2", 128, 256), X("RK2"), X("FL"), False, False)
        mm(X("PB2", 128, 256), X("M1K"), X("FL"), False, False)
        mm(X("PB2", 128, 256), X("RK1"), X("INC"), False, True)
        if t:
            ts(X("FR"), X("PB7", 128, 256), 0.0, OP.is_equal)
        tt(X("OFFP"), X("PB2", 128, 256), X("DUMPP"), OP.min)
        if t:
            ts(X("NF4"), X("PB7", 128, 256), 0.0, OP.is_gt, 4096.0, OP.mult)
        for e in range(8):
            mm(X("PB2", 256, 272), X("PL", 128 * e, 128 * e + 128), X("OFFP", e, 128, 8), e == 0, e == 7)
        tc(X("OL"), X("PB2", 256, 272))
        tc(IND(X("XW"), X("OL")), X("XF"))
        sv = X("XW", 0, 96)
        issue("g", lambda: _send(g, T, topo, core, hop, T.XR[:, 96 * t:96 * t + 96], sv[0], "xin%d" % t, "xl%d" % t),
              sv[1], [], sem="xl%d" % t, val=NE)
        if t == 0:
            consts_verdict()
        ts(X("GO"), X("OFFP"), 95.5, OP.is_ge, 4096.0, OP.mult)
        if t == 0:
            for b in range(2):
                tt(X("LG", 128 * b, 128 * b + 128), X("TR", 128 * b, 128 * b + 128), X("GO"), OP.add)
            ts(X("NF2"), X("GO"), 1.0, OP.mult)
        else:
            for b in range(2):
                tt(X("LG", 128 * b, 128 * b + 128), X("LG", 128 * b, 128 * b + 128), X("NF4"), OP.add)
                tt(X("P1", 128 * b, 128 * b + 128), X("TR", 128 * b, 128 * b + 128), X("GO"), OP.add)
            tt(X("SEL", 0, 128), V, X("VCI"), OP.subtract)
            tt(X("LG"), X("LG"), X("P1"), OP.min)
            tt(X("SEL", 0, 128), X("SEL", 0, 128), X("FR"), OP.mult)
            tt(X("NF2"), X("GO"), X("NF4"), OP.min)
        ts(X("LGU"), X("LG"), 4096.0, OP.min)
        if t:
            tt(V, X("SEL", 0, 128), X("VCI"), OP.add)
            tt(X("SEL", 128, 256), X("CAT", 128, 256), X("U1"), OP.subtract)
            tc(IND(X("D"), X("DLU", 0, 6)), X("ZER", 0, 96))
            tt(X("SEL", 128, 256), X("SEL", 128, 256), X("FR"), OP.mult)
            if t < STAGES - 1:
                ms(X("XW", 0, 96), SENT)
            tt(X("CAT", 128, 256), X("SEL", 128, 256), X("U1"), OP.add)
        else:
            act(X("CAT", 128, 256), X("U1"), AF.Copy)
            ms(X("XW", 0, 96), SENT)
        act(X("WT", 0, 128), V, AF.Square)
        act(X("WT", 128, 256), V, AF.Copy, scale=37.0)
        act(X("WT", 0, 128), X("WT", 0, 128), AF.Copy, bias=-0.25, scale=0.125)
        tt(X("WI"), X("WT", 0, 128), X("WT", 128, 256), OP.add)
        if t < STAGES - 1:
            tt(X("ZS"), X("WI"), X("S0I"), OP.add)
            ts(X("ZN"), X("ZS"), 4095, OP.bitwise_and)
        if t == 0:
            consts_back()
            consts_out()
        arrive("XR", 96 * t, 96 * t + 96, "xin%d" % t, NE)
        XR = X("XR", 96 * t, 96 * t + 96)
        Y1 = X("N3", 800, 896)
        ts(Y1, XR, 8, OP.logical_shift_right, 8191, OP.bitwise_and)
        tt(X("FX", 0, 96), Y1, X("DIAG"), OP.mult)
        scan(X("FX", 96, 192), X("HOLD"), X("FX", 0, 96), OP.mult, OP.add)
        pos = []
        o = 96
        for k in range(5):
            n = 80 - 16 * k
            ts(X("E", o, o + n), X("N3", 816 + 16 * k, 896), col("FX", 96 + 16 * k + 15), OP.is_equal)
            pos.append((o, n))
            o += n
        tt(X("E", 0, 96), Y1, X("FX", 96, 192), OP.is_equal)
        mm(X("PB4", 0, 96), X("ID"), X("OB"), True, False)
        for (o, n) in pos:
            mm(X("PB4", 96 - n, 96), X("BOK"), X("E", o, o + n), False, False)
        mm(X("PB4", 0, 96), X("BOK"), X("E", 0, 96), False, True)
        tt(X("FX", 0, 96), X("PB4", 0, 96), Y1, OP.add)
        scan(X("FX", 192, 288), X("RST"), X("FX", 0, 96), OP.max, OP.min)
        ts(X("DLU", 0, 6), S6, -1.0, OP.add)
        tc(IND(X("D"), X("DLU", 0, 6)), X("CODE"))

        def piece(q, b, k0, k1):
            o, i = X("G2", 2048 * b + 512 * k0, 2048 * b + 512 * k1), IND(X("D"), X("LGU", 128 * b + 32 * k0, 128 * b + 32 * k1))
            if q == "v":
                tc(o, i)
            else:
                act(o, i, AF.Copy)

        def sums(b, k0, k1):
            for cl in range(k0, k1):
                for m in range(8):
                    o = X("PB7", 0, 64) if b and cl == 3 else X("PB%d" % (5 + b), cl, 256, 4)
                    mm(o, X("ID"), X("G2", 2048 * b + 512 * cl + m, 2048 * b + 512 * cl + 512, 8), m == 0, m == 7)

        mm(X("PB6", 3, 256, 4), X("ID"), X("ZER", 0, 64), True, True)
        piece("v", 0, 0, 2)
        piece("s", 0, 2, 4)
        piece("v", 1, 0, 1)
        piece("s", 1, 1, 3)
        piece("s", 1, 3, 4)
        sums(0, 0, 2)
        sums(0, 2, 4)
        sums(1, 0, 1)
        sums(1, 1, 3)
        sums(1, 3, 4)
        ts(X("MS", 0, 96), XR, 21, OP.logical_shift_right)
        tt(X("FX", 0, 96), X("MS", 0, 96), X("DIAG"), OP.mult)
        scan(X("FX", 96, 192), X("HOLD"), X("FX", 0, 96), OP.mult, OP.add)
        for cl in range(1, 4):
            for p in (0, 4):
                ts(X("FX", 900 + p + cl, 948, 8), X("FX", 111, 192, 16), float(cl), OP.is_ge, 8192.0, OP.mult, waw=False)
        ts(X("FX", 990, 996), S6, 4100.0, OP.is_ge, -1.0, OP.mult)
        ts(X("N3", 896, 992), XR, 255, OP.bitwise_and)
        for b in range(2):
            ts(X("MS", 256 * b, 256 * b + 256), X("PB%d" % (5 + b), 0, 256), float(0x777777), OP.add)
            ts(X("N3", 256 * b, 256 * b + 256), X("MS", 256 * b, 256 * b + 256), 0x888888, OP.bitwise_and, 3, OP.logical_shift_right)
        tt(X("N3", 512, 768), X("N3", 0, 256), X("N3", 256, 512), OP.add)
        ts(X("P1", 0, 64), X("PB7", 0, 64), float(0x777777), OP.add)
        tt(X("MS", 0, 128), X("N3", 512, 640), X("N3", 640, 768), OP.add)
        ts(X("P1", 64, 128), X("P1", 0, 64), 0x888888, OP.bitwise_and, 3, OP.logical_shift_right)
        tt(X("MS", 128, 192), X("MS", 0, 64), X("MS", 64, 128), OP.add)
        tt(X("P1", 128, 160), X("P1", 64, 96), X("P1", 96, 128), OP.add)
        tt(X("P1", 160, 176), X("P1", 128, 144), X("P1", 144, 160), OP.add)
        tt(X("MS", 131, 192, 4), X("MS", 131, 192, 4), X("P1", 160, 176), OP.add)
        ts(X("MS", 192, 256), X("MS", 128, 192), float(0x777777), OP.add)
        ts(X("MS", 256, 320), X("MS", 192, 256), 0x888888, OP.bitwise_and, 3, OP.logical_shift_right)
        tt(X("MS", 320, 352), X("MS", 256, 288), X("MS", 288, 320), OP.add)
        tt(X("MS", 352, 368), X("MS", 320, 336), X("MS", 336, 352), OP.add)
        tt(X("MS", 368, 376), X("MS", 352, 360), X("MS", 360, 368), OP.add)
        for k in range(6):
            ts(X("MS", 384 + 8 * k, 392 + 8 * k), X("MS", 368, 376), 4 * k, OP.logical_shift_right, 15, OP.bitwise_and)
        tt(X("FX", 1000, 1048), X("MS", 384, 432), X("FX", 900, 948), OP.mult)
        scan(X("FX", 1048, 1096), X("SEG", 0, 48), X("FX", 1000, 1048), OP.mult, OP.add)
        vet = X("FX", 1055, 1096, 8)
        tt(X("DN", 0, 6), vet, X("FX", 990, 996), OP.is_equal)
        if t < STAGES - 1:
            tt(X("FX", 972, 978), vet, S6, OP.add)
        mm(X("PB4", 128, 134), X("ONE", 0, 128), X("DN", 0, 6), True, True)
        if t < STAGES - 1:
            tt(X("FX", 980, 986), X("FX", 972, 978), X("DMP6"), OP.min)
        red(col("ACOL", 0), X("PB4", 128, 134))
        if t < STAGES - 1:
            ts(X("DLU", 6, 12), X("FX", 980, 986), -1.0, OP.add)
        verdict_row(t, hop)
        tt(X("N3", 515, 768, 4), X("N3", 515, 768, 4), X("P1", 64, 128), OP.add)

    newv()
    tc(X("VHI"), X("VCI"))
    tt(X("VLO"), X("VCI"), X("VHI"), OP.subtract)
    for e in range(8):
        mm(X("PB3", 0, 16), X("PL", 128 * e, 128 * e + 128), X("VHI", e, 128, 8), e == 0, False)
        mm(X("PB3", 0, 16), X("PL", 128 * e, 128 * e + 128), X("VLO", e, 128, 8), False, e == 7)
    for k in range(6):
        hurt(k)
    thaw1()
    tc(X("FIN", 0, 16), X("PB3", 0, 16))
    tc(X("CH"), X("CAT"))
    tt(X("CL"), X("CAT"), X("CH"), OP.subtract)
    for e in range(8):
        mm(X("PB6", 256, 304), X("PL", 128 * e, 128 * e + 128), X("CH", e, 384, 8), e == 0, False)
        mm(X("PB6", 256, 304), X("PL", 128 * e, 128 * e + 128), X("CL", e, 384, 8), False, e == 7)
    tc(X("UL"), X("PB6", 256, 304))
    tt(X("FX", 288, 544), IND(X("UL", 0, 32), X("YLU", 0, 16)), X("K8T"), OP.add)
    act(X("FX", 544, 800), X("FX", 288, 544), AF.Square, scale=0.25)
    tt(X("FIN", 16, 32), X("UL", 32, 48), X("FIN", 0, 16), OP.subtract)
    tt(X("FX", 288, 544), X("FX", 544, 800), X("K2T"), OP.add)
    tt(X("MS", 0, 256), IND(X("UL", 32, 48), X("YLU", 16, 32)), X("FX", 288, 544), OP.add)
    ts(X("MS", 256, 512), X("MS", 0, 256), 4095, OP.bitwise_and)
    tc(X("YO"), X("MS", 256, 512))
    store("y", T.yt[:, :], X("YO"), "dyt")
    back(STAGES - 1)
    thaw2()
    ts(X("FR"), X("PB7", 128, 256), 0.0, OP.is_equal)
    for e in range(8):
        mm(X("PB2", 0, 16), X("PL", 128 * e, 128 * e + 128), X("FR", e, 128, 8), e == 0, e == 7)
    tc(X("YS", 16, 32), X("PB2", 0, 16))
    tt(X("FIN", 32, 48), X("FIN", 16, 32), X("YS", 16, 32), OP.mult)
    tt(X("YS", 0, 16), X("FIN", 32, 48), X("FIN", 0, 16), OP.add)
    store("y", T.ys[:, :], X("YS"), "dys")

    for n, v in [("dx", 16), ("dsd", 16), ("dv0", 16), ("dth", 16), ("dyt", 16), ("dys", 16)]:
        g.wait_ge(T.sem[n], v)
    for q in "vspg":
        g.wait_ge(T.sem["q" + q], CNT[q])
    for t in range(STAGES):
        for n in ("xin", "rin", "xl", "rl"):
            g.wait_ge(T.sem[n + str(t)], NE)
